import numpy as np
import ml_dtypes


def mxq(x, axis, fmt="e4m3"):
    dtype, down = {"e4m3": (ml_dtypes.float8_e4m3fn, 7), "e5m2": (ml_dtypes.float8_e5m2, 14)}[fmt]
    v = np.moveaxis(np.asarray(x, np.float32).astype(ml_dtypes.bfloat16).astype(np.float64), axis, -1)
    blocks = v.reshape(v.shape[:-1] + (-1, 32))
    amax = np.abs(blocks).max(-1, keepdims=True)
    byte = np.maximum(np.where(amax > 0, np.frexp(amax)[1] - 1 + 127, 0) - down, 1)
    scale = np.exp2(byte - 127.0)
    codes = (blocks / scale).astype(np.float32).astype(dtype).astype(np.float64)
    return np.moveaxis((codes * scale).reshape(v.shape), -1, axis)


WIDE = False


def mx_kscale(k):
    if not WIDE:
        return np.ones(k)
    levels = np.array([10, -10, 5, -5, 0])
    if k % 512:
        return np.exp2(np.random.permutation(np.resize(levels, k // 32))).repeat(32)
    a = np.empty((k // 512, 16))
    for p in range(k // 512):
        a[p, :8] = np.random.permutation(np.resize(levels, 8))
        for g in range(8):
            far = levels[np.abs(levels - a[p, g]) >= 10]
            a[p, g + 8] = far[np.random.randint(len(far))]
    return np.exp2(a.ravel()).repeat(32)


def f64(x):
    return np.asarray(x).astype(np.float64)


def striped(idx):
    return np.tile(idx.reshape(-1, 16).T, (8, 1)).astype(np.uint16)


def unstriped(offs):
    return offs[:16].T.reshape(-1).astype(np.int64)


def pack_weight(w):
    k, n = w.shape
    w = f64(np.asarray(w, np.float32).astype(ml_dtypes.bfloat16)).reshape(k // 32, 32, n)
    amax = np.abs(w).max(1)
    byte = np.clip(np.where(amax > 0, np.frexp(amax)[1] - 1 + 127 - 7, 1), 1, 254)
    scaled = (w * np.exp2(127.0 - byte)[:, None, :]).reshape(k, n).astype(np.float32)
    words = np.ascontiguousarray(scaled.reshape(k // 512, 128, 4, n).transpose(0, 1, 3, 2)).astype(ml_dtypes.float8_e4m3fn).view(np.uint8)
    return words, np.ascontiguousarray(byte.astype(np.uint8).reshape(k // 512, 16, n))


def unpack_weight(words, scales):
    g, p, n, _ = words.shape
    vals = np.ascontiguousarray(words).view(ml_dtypes.float8_e4m3fn).astype(np.float64) * np.repeat(np.exp2(scales.astype(np.float64) - 127.0), 8, axis=1)[..., None]
    return vals.transpose(0, 1, 3, 2).reshape(g * 512, n)


def sigmoid(v):
    return 1.0 / (1.0 + np.exp(-np.maximum(v, -700.0)))


K, T, S, H, V, W = 1024, 1024, 512, 512, 512, 2048


def setup_inputs():
    n = np.random.standard_normal
    s = mx_kscale(K)[:, None]
    u = mx_kscale(H)
    packed_xT = pack_weight(n((K, T)) * s)
    packed_eT = pack_weight(n((H, W)) / np.sqrt(H) / u[:, None])
    return {
        "x_words": packed_xT[0],
        "x_scales": packed_xT[1],
        "w1": (n((K, H)) / np.sqrt(K) / s * u).astype(np.float32),
        "e_words": packed_eT[0],
        "e_scales": packed_eT[1],
        "lab": (np.where(np.random.uniform(size=(S, V)) < 0.3, 1.0, -1.0)).astype(np.float32),
        "offs": striped(np.random.permutation(T)[:S]),
        "txt": striped(np.random.permutation(W)[:V]),
    }


def reference(x_words, x_scales, w1, e_words, e_scales, lab, offs, txt):
    xq = unpack_weight(x_words, x_scales)[:, unstriped(offs)]
    h = mxq(f64(w1), 0, "e4m3").T @ xq
    e_txt = unpack_weight(e_words, e_scales)[:, unstriped(txt)]
    y = mxq(h, 0, "e4m3").T @ e_txt
    z = f64(lab) * (1.5 * y - 0.5)
    return f64(lab) * (-1.5 * sigmoid(-1.0 * z))

@@ -1,0 +1,136 @@
+from contextlib import ExitStack
+
+import concourse.mybir as mybir
+
+K, T, S, H, V, W = 1024, 1024, 512, 512, 512, 2048
+FLOPS = 2 * K * H * S + 2 * H * S * V
+
+F32 = mybir.dt.float32
+BF16 = mybir.dt.bfloat16
+I32 = mybir.dt.int32
+U32 = mybir.dt.uint32
+U16 = mybir.dt.uint16
+U8 = mybir.dt.uint8
+FP8X4 = mybir.dt.float8_e4m3fn_x4
+ALU = mybir.AluOpType
+ACT = mybir.ActivationFunctionType
+
+P = 128
+PACK = 4
+PASSES = K // (P * PACK)
+CHUNKS = S // P
+LCOL = P // 16
+SCALAR_M = [64, 64]
+
+
+def tile_picked_ysiglip_grad_p_kernel(tc, x_words, x_scales, w1, e_words, e_scales, lab, offs, txt, out):
+    nc = tc.nc
+    with ExitStack() as ctx:
+        keep = ctx.enter_context(tc.tile_pool(name="keep", bufs=1))
+        psum = ctx.enter_context(tc.psum_pool(name="psum", bufs=1))
+
+        offs_t = keep.tile([P, S // 16], U16, name="offs_t")
+        txt_t = keep.tile([P, V // 16], U16, name="txt_t")
+        xs_tab = keep.tile([P, T], U8, name="xs_tab", align_bytes=64)
+        es_tab = keep.tile([P, W], U8, name="es_tab", align_bytes=64)
+        xw_tab = [keep.tile([P, T], I32, name=f"xw_tab{o}", align_bytes=64) for o in range(PASSES)]
+        ew_tab = keep.tile([P, W], I32, name="ew_tab", align_bytes=64)
+        w_raw = [keep.tile([P, PACK, H], F32, name=f"w_raw{o}", align_bytes=64) for o in range(PASSES)]
+        lab_t = [keep.tile([P, V], F32, name=f"lab{c}", align_bytes=64) for c in range(CHUNKS)]
+
+        nc.vector.memset(es_tab[:].bitcast(I32), 0)
+        nc.gpsimd.memset(xs_tab[:].bitcast(I32), 0)
+
+        def load_w(o):
+            rows = w1[o * P * PACK : (o + 1) * P * PACK, :]
+            nc.sync.dma_start(out=w_raw[o][:], in_=rows.rearrange("(p r) c -> p r c", r=PACK))
+
+        load_w(0)
+        nc.sync.dma_start(txt_t[:], txt)
+        for q in range(4):
+            nc.sync.dma_start(out=es_tab[32 * q : 32 * q + 4, :].bitcast(I32), in_=e_scales[0, 4 * q : 4 * q + 4, :].bitcast(I32))
+        nc.sync.dma_start(offs_t[:], offs)
+        for q in range(4):
+            nc.gpsimd.dma_start(out=xs_tab[32 * q : 32 * q + 4 * PASSES, :].bitcast(I32), in_=x_scales[:, 4 * q : 4 * q + 4, :].bitcast(I32))
+        load_w(1)
+        for o in range(PASSES):
+            nc.sync.dma_start(out=xw_tab[o][:], in_=x_words[o].rearrange("p n t -> p (n t)").bitcast(I32))
+        nc.sync.dma_start(out=ew_tab[:], in_=e_words[0].rearrange("p n t -> p (n t)").bitcast(I32))
+        for c in range(CHUNKS):
+            nc.sync.dma_start(out=lab_t[c][:], in_=lab[c * P : (c + 1) * P, :])
+
+        es = keep.tile([P, V], U8, name="es", align_bytes=64)
+        nc.vector.tensor_copy(es[:], es_tab[:].indirect(txt_t[:]))
+
+        w_codes, w_scales = [], []
+        xs = keep.tile([P, S], U8, name="xs", align_bytes=64)
+        for o in range(PASSES):
+            w_bf = keep.tile([P, PACK * H], BF16, name=f"w_bf{o}", align_bytes=64)
+            dst = w_bf[:].rearrange("p (t m r) -> p m r t", t=PACK, r=PACK)
+            src = w_raw[o][:].rearrange("p r (m t) -> p m r t", t=PACK)
+            sm = SCALAR_M[o]
+            nc.scalar.copy(out=dst[:, :sm], in_=src[:, :sm])
+            if sm < P:
+                nc.vector.tensor_copy(out=dst[:, sm:], in_=src[:, sm:])
+            if o == 0:
+                nc.vector.tensor_copy(xs[:], xs_tab[:].indirect(offs_t[:]))
+            codes = keep.tile([P, H], U32, name=f"w_codes{o}", align_bytes=64)
+            scales = keep.tile([P, H], U8, name=f"w_scales{o}", align_bytes=64)
+            nc.vector.quantize_mx(out=codes[:].bitcast(FP8X4), scales=scales[:], in_=w_bf[:])
+            w_codes.append(codes)
+            w_scales.append(scales)
+
+        x0 = keep.tile([P, S], U32, name="x0", align_bytes=64)
+        nc.vector.tensor_copy(x0[:], xw_tab[0][:].bitcast(U32).indirect(offs_t[:]))
+        x1 = []
+        for c in range(CHUNKS):
+            g = keep.tile([P, P], U32, name=f"x1_{c}", align_bytes=64)
+            nc.vector.tensor_copy(g[:], xw_tab[1][:].bitcast(U32).indirect(offs_t[:, c * LCOL : (c + 1) * LCOL]))
+            x1.append(g)
+
+        h_codes, h_scales = [], []
+        for c in range(CHUNKS):
+            cols = slice(c * P, (c + 1) * P)
+            acc = psum.tile([P, PACK, P], F32, name=f"h_acc{c}")
+            for t in range(PACK):
+                wcols = slice(t * P, (t + 1) * P)
+                for o in range(PASSES):
+                    rhs = x0[:, cols] if o == 0 else x1[c][:]
+                    nc.tensor.matmul_mx(
+                        out=acc[:, t, :],
+                        lhsT=w_codes[o][:, wcols].bitcast(FP8X4),
+                        lhsT_scale=w_scales[o][:, wcols],
+                        rhs=rhs.bitcast(FP8X4),
+                        rhs_scale=xs[4 * o : P, cols],
+                        start=(o == 0),
+                        stop=(o == PASSES - 1),
+                    )
+            h_bf = keep.tile([P, P, PACK], BF16, name=f"h_bf{c}", align_bytes=64)
+            nc.scalar.copy(out=h_bf[:], in_=acc[:].rearrange("p t n -> p n t"))
+            codes = keep.tile([P, P], U32, name=f"h_codes{c}", align_bytes=64)
+            scales = keep.tile([P, P], U8, name=f"h_scales{c}", align_bytes=64)
+            nc.vector.quantize_mx(out=codes[:].bitcast(FP8X4), scales=scales[:], in_=h_bf[:].rearrange("p n t -> p (n t)"))
+            h_codes.append(codes)
+            h_scales.append(scales)
+
+        ew = keep.tile([P, V], U32, name="ew", align_bytes=64)
+        nc.vector.tensor_copy(ew[:], ew_tab[:].bitcast(U32).indirect(txt_t[:]))
+
+        for c in range(CHUNKS):
+            y = psum.tile([P, V], F32, name=f"y{c}")
+            nc.tensor.matmul_mx(
+                out=y[:],
+                lhsT=h_codes[c][:].bitcast(FP8X4),
+                lhsT_scale=h_scales[c][:],
+                rhs=ew[:].bitcast(FP8X4),
+                rhs_scale=es[:],
+                start=True,
+                stop=True,
+            )
+            shift = keep.tile([P, V], F32, name=f"shift{c}", align_bytes=64)
+            nc.vector.tensor_scalar(out=shift[:], in0=lab_t[c][:], scalar1=0.75, scalar2=None, op0=ALU.mult)
+            th = keep.tile([P, V], F32, name=f"th{c}", align_bytes=64)
+            nc.scalar.activation(out=th[:], in_=y[:], func=ACT.Tanh, bias=-0.25, scale=0.75)
+            res = keep.tile([P, V], F32, name=f"res{c}", align_bytes=64)
+            nc.vector.scalar_tensor_tensor(out=res[:], in0=th[:], scalar=0.75, in1=shift[:], op0=ALU.mult, op1=ALU.subtract)
+            nc.sync.dma_start(out=out[c * P : (c + 1) * P, :], in_=res[:])

@@ -20,7 +20,7 @@ PACK = 4
 PASSES = K // (P * PACK)
 CHUNKS = S // P
 LCOL = P // 16
-SCALAR_M = [64, 64]
+SCALAR_M = [96, 64]
 
 
 def tile_picked_ysiglip_grad_p_kernel(tc, x_words, x_scales, w1, e_words, e_scales, lab, offs, txt, out):
@@ -32,40 +32,50 @@ def tile_picked_ysiglip_grad_p_kernel(tc, x_words, x_scales, w1, e_words, e_scal
         offs_t = keep.tile([P, S // 16], U16, name="offs_t")
         txt_t = keep.tile([P, V // 16], U16, name="txt_t")
         xs_tab = keep.tile([P, T], U8, name="xs_tab", align_bytes=64)
-        es_tab = keep.tile([P, W], U8, name="es_tab", align_bytes=64)
-        xw_tab = [keep.tile([P, T], I32, name=f"xw_tab{o}", align_bytes=64) for o in range(PASSES)]
-        ew_tab = keep.tile([P, W], I32, name="ew_tab", align_bytes=64)
-        w_raw = [keep.tile([P, PACK, H], F32, name=f"w_raw{o}", align_bytes=64) for o in range(PASSES)]
-        lab_t = [keep.tile([P, V], F32, name=f"lab{c}", align_bytes=64) for c in range(CHUNKS)]
+        es_tab = keep.tile([P, W], U8, name="es_tab", tag="wc0", align_bytes=64)
 
+        nc.vector.memset(xs_tab[:].bitcast(I32), 0)
         nc.vector.memset(es_tab[:].bitcast(I32), 0)
-        nc.gpsimd.memset(xs_tab[:].bitcast(I32), 0)
+        warm = keep.tile([P, 8], F32, name="warm", tag="big1", align_bytes=64)
+        nc.vector.memset(warm[:], 0.0)
+        warm_out = keep.tile([P, 8], F32, name="warm_out", tag="xw1", align_bytes=64)
+        nc.scalar.activation(out=warm_out[:], in_=warm[:], func=ACT.Tanh, bias=-0.25, scale=0.75)
+        xw_tab = [keep.tile([P, T], I32, name=f"xw_tab{o}", tag=f"xw{o}", align_bytes=64) for o in range(PASSES)]
+        w_raw = [keep.tile([P, PACK, H], F32, name=f"w_raw{o}", tag=f"big{o}", align_bytes=64) for o in range(PASSES)]
 
         def load_w(o):
             rows = w1[o * P * PACK : (o + 1) * P * PACK, :]
             nc.sync.dma_start(out=w_raw[o][:], in_=rows.rearrange("(p r) c -> p r c", r=PACK))
 
-        load_w(0)
-        nc.sync.dma_start(txt_t[:], txt)
-        for q in range(4):
-            nc.sync.dma_start(out=es_tab[32 * q : 32 * q + 4, :].bitcast(I32), in_=e_scales[0, 4 * q : 4 * q + 4, :].bitcast(I32))
-        nc.sync.dma_start(offs_t[:], offs)
-        for q in range(4):
-            nc.gpsimd.dma_start(out=xs_tab[32 * q : 32 * q + 4 * PASSES, :].bitcast(I32), in_=x_scales[:, 4 * q : 4 * q + 4, :].bitcast(I32))
-        load_w(1)
-        for o in range(PASSES):
+        def load_x(o):
             nc.sync.dma_start(out=xw_tab[o][:], in_=x_words[o].rearrange("p n t -> p (n t)").bitcast(I32))
-        nc.sync.dma_start(out=ew_tab[:], in_=e_words[0].rearrange("p n t -> p (n t)").bitcast(I32))
-        for c in range(CHUNKS):
-            nc.sync.dma_start(out=lab_t[c][:], in_=lab[c * P : (c + 1) * P, :])
 
-        es = keep.tile([P, V], U8, name="es", align_bytes=64)
-        nc.vector.tensor_copy(es[:], es_tab[:].indirect(txt_t[:]))
+        def load_xs():
+            for q in range(4):
+                nc.sync.dma_start(out=xs_tab[32 * q : 32 * q + 4 * PASSES, :].bitcast(I32), in_=x_scales[:, 4 * q : 4 * q + 4, :].bitcast(I32))
+
+        def load_es():
+            for q in range(4):
+                nc.sync.dma_start(out=es_tab[32 * q : 32 * q + 4, :].bitcast(I32), in_=e_scales[0, 4 * q : 4 * q + 4, :].bitcast(I32))
+
+        nc.sync.dma_start(offs_t[:], offs)
+        nc.sync.dma_start(txt_t[:], txt)
+        load_x(0)
+        load_xs()
+        load_w(0)
+        load_es()
+        load_w(1)
+        load_x(1)
+
+        xs = keep.tile([P, S], U8, name="xs", align_bytes=64)
+        nc.vector.tensor_copy(xs[:], xs_tab[:].indirect(offs_t[:]))
+        x0 = keep.tile([P, S], U32, name="x0", align_bytes=64)
+        nc.vector.tensor_copy(x0[:], xw_tab[0][:].bitcast(U32).indirect(offs_t[:]))
 
         w_codes, w_scales = [], []
-        xs = keep.tile([P, S], U8, name="xs", align_bytes=64)
+        es = keep.tile([P, V], U8, name="es", align_bytes=64)
         for o in range(PASSES):
-            w_bf = keep.tile([P, PACK * H], BF16, name=f"w_bf{o}", align_bytes=64)
+            w_bf = keep.tile([P, PACK * H], BF16, name=f"w_bf{o}", tag=f"wbf{o}", align_bytes=64)
             dst = w_bf[:].rearrange("p (t m r) -> p m r t", t=PACK, r=PACK)
             src = w_raw[o][:].rearrange("p r (m t) -> p m r t", t=PACK)
             sm = SCALAR_M[o]
@@ -73,64 +83,93 @@ def tile_picked_ysiglip_grad_p_kernel(tc, x_words, x_scales, w1, e_words, e_scal
             if sm < P:
                 nc.vector.tensor_copy(out=dst[:, sm:], in_=src[:, sm:])
             if o == 0:
-                nc.vector.tensor_copy(xs[:], xs_tab[:].indirect(offs_t[:]))
-            codes = keep.tile([P, H], U32, name=f"w_codes{o}", align_bytes=64)
+                nc.vector.tensor_copy(es[:], es_tab[:].indirect(txt_t[:]))
+            codes = keep.tile([P, H], U32, name=f"w_codes{o}", tag=f"wc{o}", align_bytes=64)
             scales = keep.tile([P, H], U8, name=f"w_scales{o}", align_bytes=64)
-            nc.vector.quantize_mx(out=codes[:].bitcast(FP8X4), scales=scales[:], in_=w_bf[:])
+            if o == 1:
+                x1_first = keep.tile([P, P], U32, name="x1_first", align_bytes=64)
+                nc.vector.tensor_copy(x1_first[:], xw_tab[1][:].bitcast(U32).indirect(offs_t[:, 0:LCOL]))
+            pieces = 1 if o == 0 else 4
+            for i in range(pieces):
+                n = H // pieces
+                nc.vector.quantize_mx(out=codes[:, i * n : (i + 1) * n].bitcast(FP8X4), scales=scales[:, i * n : (i + 1) * n], in_=w_bf[:, i * n * PACK : (i + 1) * n * PACK])
             w_codes.append(codes)
             w_scales.append(scales)
 
-        x0 = keep.tile([P, S], U32, name="x0", align_bytes=64)
-        nc.vector.tensor_copy(x0[:], xw_tab[0][:].bitcast(U32).indirect(offs_t[:]))
-        x1 = []
-        for c in range(CHUNKS):
-            g = keep.tile([P, P], U32, name=f"x1_{c}", align_bytes=64)
-            nc.vector.tensor_copy(g[:], xw_tab[1][:].bitcast(U32).indirect(offs_t[:, c * LCOL : (c + 1) * LCOL]))
+        ew_tab = keep.tile([P, W], I32, name="ew_tab", tag="xw0", align_bytes=64)
+        nc.sync.dma_start(out=ew_tab[:], in_=e_words[0].rearrange("p n t -> p (n t)").bitcast(I32))
+        lab_pairs = []
+        for half in range(2):
+            pair = keep.tile([P, 2, V], F32, name=f"lab{half}", tag=f"big{half}", align_bytes=64)
+            for i in range(2):
+                c = 2 * half + i
+                nc.sync.dma_start(out=pair[:, i, :], in_=lab[c * P : (c + 1) * P, :])
+            lab_pairs.append(pair)
+
+        x1 = [x1_first[:]]
+        x1_rest = keep.tile([P, S - P], U32, name="x1_rest", tag="wbf1", align_bytes=64)
+        for c in range(1, CHUNKS):
+            g = x1_rest[:, (c - 1) * P : c * P]
+            nc.vector.tensor_copy(g, xw_tab[1][:].bitcast(U32).indirect(offs_t[:, c * LCOL : (c + 1) * LCOL]))
             x1.append(g)
 
-        h_codes, h_scales = [], []
-        for c in range(CHUNKS):
+        ew = keep.tile([P, V], U32, name="ew", align_bytes=64)
+        h_acc = [psum.tile([P, PACK, P], F32, name=f"h_acc{c}") for c in range(CHUNKS)]
+
+        def project(c, t, o):
             cols = slice(c * P, (c + 1) * P)
-            acc = psum.tile([P, PACK, P], F32, name=f"h_acc{c}")
+            wcols = slice(t * P, (t + 1) * P)
+            rhs = x0[:, cols] if o == 0 else x1[c]
+            nc.tensor.matmul_mx(
+                out=h_acc[c][:, t, :],
+                lhsT=w_codes[o][:, wcols].bitcast(FP8X4),
+                lhsT_scale=w_scales[o][:, wcols],
+                rhs=rhs.bitcast(FP8X4),
+                rhs_scale=xs[4 * o : P, cols],
+                start=(o == 0),
+                stop=(o == PASSES - 1),
+            )
+
+        y_acc = [psum.tile([P, V], F32, name=f"y{c}") for c in range(CHUNKS)]
+        for c in range(CHUNKS):
+            project(c, 0, 0)
+        h_codes, h_scales, shifts = [], [], []
+        for c in range(CHUNKS):
+            acc = h_acc[c]
             for t in range(PACK):
-                wcols = slice(t * P, (t + 1) * P)
                 for o in range(PASSES):
-                    rhs = x0[:, cols] if o == 0 else x1[c][:]
-                    nc.tensor.matmul_mx(
-                        out=acc[:, t, :],
-                        lhsT=w_codes[o][:, wcols].bitcast(FP8X4),
-                        lhsT_scale=w_scales[o][:, wcols],
-                        rhs=rhs.bitcast(FP8X4),
-                        rhs_scale=xs[4 * o : P, cols],
-                        start=(o == 0),
-                        stop=(o == PASSES - 1),
-                    )
-            h_bf = keep.tile([P, P, PACK], BF16, name=f"h_bf{c}", align_bytes=64)
+                    if (t, o) != (0, 0):
+                        project(c, t, o)
+            h_bf = keep.tile([P, P, PACK], BF16, name=f"h_bf{c}", tag=f"hbf{c}", align_bytes=64)
             nc.scalar.copy(out=h_bf[:], in_=acc[:].rearrange("p t n -> p n t"))
-            codes = keep.tile([P, P], U32, name=f"h_codes{c}", align_bytes=64)
+            if c == 0:
+                nc.vector.tensor_copy(ew[:], ew_tab[:].bitcast(U32).indirect(txt_t[:]))
+                first_codes = keep.tile([P, 2 * P], U32, name="first_codes", tag="xw0", align_bytes=64)
+            if c < 2:
+                codes = first_codes[:, c * P : (c + 1) * P]
+            else:
+                shift = keep.tile([P, 2, V], F32, name=f"shift{c}", align_bytes=64)
+                nc.vector.tensor_scalar(out=shift[:], in0=lab_pairs[c - 2][:], scalar1=0.75, scalar2=None, op0=ALU.mult)
+                shifts.extend([shift[:, 0, :], shift[:, 1, :]])
+                codes = keep.tile([P, P], U32, name=f"late_codes{c}", tag=f"big{c - 2}", align_bytes=64)[:]
             scales = keep.tile([P, P], U8, name=f"h_scales{c}", align_bytes=64)
-            nc.vector.quantize_mx(out=codes[:].bitcast(FP8X4), scales=scales[:], in_=h_bf[:].rearrange("p n t -> p (n t)"))
+            nc.vector.quantize_mx(out=codes.bitcast(FP8X4), scales=scales[:], in_=h_bf[:].rearrange("p n t -> p (n t)"))
             h_codes.append(codes)
             h_scales.append(scales)
 
-        ew = keep.tile([P, V], U32, name="ew", align_bytes=64)
-        nc.vector.tensor_copy(ew[:], ew_tab[:].bitcast(U32).indirect(txt_t[:]))
-
+        res = keep.tile([P, CHUNKS, V], F32, name="res", tag=f"hbf{CHUNKS - 1}", align_bytes=64)
         for c in range(CHUNKS):
-            y = psum.tile([P, V], F32, name=f"y{c}")
+            y = y_acc[c]
             nc.tensor.matmul_mx(
                 out=y[:],
-                lhsT=h_codes[c][:].bitcast(FP8X4),
+                lhsT=h_codes[c].bitcast(FP8X4),
                 lhsT_scale=h_scales[c][:],
                 rhs=ew[:].bitcast(FP8X4),
                 rhs_scale=es[:],
                 start=True,
                 stop=True,
             )
-            shift = keep.tile([P, V], F32, name=f"shift{c}", align_bytes=64)
-            nc.vector.tensor_scalar(out=shift[:], in0=lab_t[c][:], scalar1=0.75, scalar2=None, op0=ALU.mult)
             th = keep.tile([P, V], F32, name=f"th{c}", align_bytes=64)
             nc.scalar.activation(out=th[:], in_=y[:], func=ACT.Tanh, bias=-0.25, scale=0.75)
-            res = keep.tile([P, V], F32, name=f"res{c}", align_bytes=64)
-            nc.vector.scalar_tensor_tensor(out=res[:], in0=th[:], scalar=0.75, in1=shift[:], op0=ALU.mult, op1=ALU.subtract)
-            nc.sync.dma_start(out=out[c * P : (c + 1) * P, :], in_=res[:])
+            nc.vector.scalar_tensor_tensor(out=res[:, c, :], in0=th[:], scalar=0.75, in1=shifts[c], op0=ALU.mult, op1=ALU.subtract)
+            nc.sync.dma_start(out=out[c * P : (c + 1) * P, :], in_=res[:, c, :])

@@ -56,7 +56,7 @@ def tile_picked_ysiglip_grad_p_kernel(tc, x_words, x_scales, w1, e_words, e_scal
 
         def load_es():
             for q in range(4):
-                nc.sync.dma_start(out=es_tab[32 * q : 32 * q + 4, :].bitcast(I32), in_=e_scales[0, 4 * q : 4 * q + 4, :].bitcast(I32))
+                nc.sync.dma_start(out=es_tab[q:P:32, :].bitcast(I32), in_=e_scales[0, q:16:4, :].bitcast(I32))
 
         nc.sync.dma_start(offs_t[:], offs)
         nc.sync.dma_start(txt_t[:], txt)
@@ -76,8 +76,8 @@ def tile_picked_ysiglip_grad_p_kernel(tc, x_words, x_scales, w1, e_words, e_scal
         es = keep.tile([P, V], U8, name="es", align_bytes=64)
         for o in range(PASSES):
             w_bf = keep.tile([P, PACK * H], BF16, name=f"w_bf{o}", tag=f"wbf{o}", align_bytes=64)
-            dst = w_bf[:].rearrange("p (t m r) -> p m r t", t=PACK, r=PACK)
-            src = w_raw[o][:].rearrange("p r (m t) -> p m r t", t=PACK)
+            dst = w_bf[:].rearrange("p (t m r) -> p m t r", t=PACK, r=PACK)
+            src = w_raw[o][:].rearrange("p r (m t) -> p m t r", t=PACK)
             sm = SCALAR_M[o]
             nc.scalar.copy(out=dst[:, :sm], in_=src[:, :sm])
             if sm < P:
@@ -131,6 +131,16 @@ def tile_picked_ysiglip_grad_p_kernel(tc, x_words, x_scales, w1, e_words, e_scal
             )
 
         y_acc = [psum.tile([P, V], F32, name=f"y{c}") for c in range(CHUNKS)]
+        for i in range(3):
+            nc.tensor.matmul_mx(
+                out=y_acc[CHUNKS - 1 - i][:],
+                lhsT=w_codes[0][:, 0:P].bitcast(FP8X4),
+                lhsT_scale=w_scales[0][:, 0:P],
+                rhs=x0[:].bitcast(FP8X4),
+                rhs_scale=xs[:],
+                start=True,
+                stop=True,
+            )
         for c in range(CHUNKS):
             project(c, 0, 0)
         h_codes, h_scales, shifts = [], [], []
@@ -144,21 +154,19 @@ def tile_picked_ysiglip_grad_p_kernel(tc, x_words, x_scales, w1, e_words, e_scal
             nc.scalar.copy(out=h_bf[:], in_=acc[:].rearrange("p t n -> p n t"))
             if c == 0:
                 nc.vector.tensor_copy(ew[:], ew_tab[:].bitcast(U32).indirect(txt_t[:]))
-                first_codes = keep.tile([P, 2 * P], U32, name="first_codes", tag="xw0", align_bytes=64)
-            if c < 2:
-                codes = first_codes[:, c * P : (c + 1) * P]
-            else:
-                shift = keep.tile([P, 2, V], F32, name=f"shift{c}", align_bytes=64)
-                nc.vector.tensor_scalar(out=shift[:], in0=lab_pairs[c - 2][:], scalar1=0.75, scalar2=None, op0=ALU.mult)
-                shifts.extend([shift[:, 0, :], shift[:, 1, :]])
-                codes = keep.tile([P, P], U32, name=f"late_codes{c}", tag=f"big{c - 2}", align_bytes=64)[:]
+                all_codes = keep.tile([P, S], U32, name="all_codes", tag="xw0", align_bytes=64)
+            codes = all_codes[:, c * P : (c + 1) * P]
             scales = keep.tile([P, P], U8, name=f"h_scales{c}", align_bytes=64)
             nc.vector.quantize_mx(out=codes.bitcast(FP8X4), scales=scales[:], in_=h_bf[:].rearrange("p n t -> p (n t)"))
             h_codes.append(codes)
             h_scales.append(scales)
 
-        res = keep.tile([P, CHUNKS, V], F32, name="res", tag=f"hbf{CHUNKS - 1}", align_bytes=64)
+        res = keep.tile([P, CHUNKS, V], F32, name="res", align_bytes=64)
         for c in range(CHUNKS):
+            if c < 2:
+                shift = keep.tile([P, 2, V], F32, name=f"shift{c}", align_bytes=64)
+                nc.vector.tensor_scalar(out=shift[:], in0=lab_pairs[c][:], scalar1=0.75, scalar2=None, op0=ALU.mult)
+                shifts.extend([shift[:, 0, :], shift[:, 1, :]])
             y = y_acc[c]
             nc.tensor.matmul_mx(
                 out=y[:],

@@ -17,10 +17,16 @@ ACT = mybir.ActivationFunctionType
 
 P = 128
 PACK = 4
+QUAD = 32
+QUADS = P // QUAD
+ROWS = 4
+LIST = 16
+ALIGN = 64
 PASSES = K // (P * PACK)
 CHUNKS = S // P
-LCOL = P // 16
-SCALAR_M = [96, 64]
+PAIR = 2
+SCALAR_GROUPS = (96, 64)
+LAST_PARTS = 2
 
 
 def tile_picked_ysiglip_grad_p_kernel(tc, x_words, x_scales, w1, e_words, e_scales, lab, offs, txt, out):
@@ -29,19 +35,16 @@ def tile_picked_ysiglip_grad_p_kernel(tc, x_words, x_scales, w1, e_words, e_scal
         keep = ctx.enter_context(tc.tile_pool(name="keep", bufs=1))
         psum = ctx.enter_context(tc.psum_pool(name="psum", bufs=1))
 
-        offs_t = keep.tile([P, S // 16], U16, name="offs_t")
-        txt_t = keep.tile([P, V // 16], U16, name="txt_t")
-        xs_tab = keep.tile([P, T], U8, name="xs_tab", align_bytes=64)
-        es_tab = keep.tile([P, W], U8, name="es_tab", tag="wc0", align_bytes=64)
+        offs_t = keep.tile([P, S // LIST], U16, name="offs_t")
+        txt_t = keep.tile([P, V // LIST], U16, name="txt_t")
 
+        xs_tab = keep.tile([P, T], U8, name="xs_tab", align_bytes=ALIGN)
+        es_tab = keep.tile([P, W], U8, name="es_tab", tag="w_codes0", align_bytes=ALIGN)
         nc.vector.memset(xs_tab[:].bitcast(I32), 0)
-        nc.vector.memset(es_tab[:].bitcast(I32), 0)
-        warm = keep.tile([P, 8], F32, name="warm", tag="big1", align_bytes=64)
-        nc.vector.memset(warm[:], 0.0)
-        warm_out = keep.tile([P, 8], F32, name="warm_out", tag="xw1", align_bytes=64)
-        nc.scalar.activation(out=warm_out[:], in_=warm[:], func=ACT.Tanh, bias=-0.25, scale=0.75)
-        xw_tab = [keep.tile([P, T], I32, name=f"xw_tab{o}", tag=f"xw{o}", align_bytes=64) for o in range(PASSES)]
-        w_raw = [keep.tile([P, PACK, H], F32, name=f"w_raw{o}", tag=f"big{o}", align_bytes=64) for o in range(PASSES)]
+        nc.gpsimd.memset(es_tab[:].bitcast(I32), 0)
+
+        xw_tab = [keep.tile([P, T], I32, name=f"xw_tab{o}", tag=f"words{o}", align_bytes=ALIGN) for o in range(PASSES)]
+        w_raw = [keep.tile([P, PACK, H], F32, name=f"w_raw{o}", tag=f"floats{o}", align_bytes=ALIGN) for o in range(PASSES)]
 
         def load_w(o):
             rows = w1[o * P * PACK : (o + 1) * P * PACK, :]
@@ -50,134 +53,142 @@ def tile_picked_ysiglip_grad_p_kernel(tc, x_words, x_scales, w1, e_words, e_scal
         def load_x(o):
             nc.sync.dma_start(out=xw_tab[o][:], in_=x_words[o].rearrange("p n t -> p (n t)").bitcast(I32))
 
-        def load_xs():
-            for q in range(4):
-                nc.sync.dma_start(out=xs_tab[32 * q : 32 * q + 4 * PASSES, :].bitcast(I32), in_=x_scales[:, 4 * q : 4 * q + 4, :].bitcast(I32))
-
-        def load_es():
-            for q in range(4):
-                nc.sync.dma_start(out=es_tab[q:P:32, :].bitcast(I32), in_=e_scales[0, q:16:4, :].bitcast(I32))
-
         nc.sync.dma_start(offs_t[:], offs)
-        nc.sync.dma_start(txt_t[:], txt)
         load_x(0)
-        load_xs()
+        nc.sync.dma_start(txt_t[:], txt)
+        for q in range(QUADS):
+            nc.sync.dma_start(
+                out=xs_tab[QUAD * q : QUAD * q + ROWS * PASSES, :].bitcast(I32),
+                in_=x_scales[:, ROWS * q : ROWS * (q + 1), :].bitcast(I32),
+            )
         load_w(0)
-        load_es()
+        for r in range(ROWS):
+            nc.sync.dma_start(
+                out=es_tab[r:P:QUAD, :].bitcast(I32),
+                in_=e_scales[0, r : ROWS * QUADS : ROWS, :].bitcast(I32),
+            )
         load_w(1)
         load_x(1)
 
-        xs = keep.tile([P, S], U8, name="xs", align_bytes=64)
+        xs = keep.tile([P, S], U8, name="xs", align_bytes=ALIGN)
         nc.vector.tensor_copy(xs[:], xs_tab[:].indirect(offs_t[:]))
-        x0 = keep.tile([P, S], U32, name="x0", align_bytes=64)
+        x0 = keep.tile([P, S], U32, name="x0", align_bytes=ALIGN)
         nc.vector.tensor_copy(x0[:], xw_tab[0][:].bitcast(U32).indirect(offs_t[:]))
 
-        w_codes, w_scales = [], []
-        es = keep.tile([P, V], U8, name="es", align_bytes=64)
-        for o in range(PASSES):
-            w_bf = keep.tile([P, PACK * H], BF16, name=f"w_bf{o}", tag=f"wbf{o}", align_bytes=64)
+        def round_w(o):
+            w_bf = keep.tile([P, PACK * H], BF16, name=f"w_bf{o}", tag=f"w_bf{o}", align_bytes=ALIGN)
             dst = w_bf[:].rearrange("p (t m r) -> p m t r", t=PACK, r=PACK)
             src = w_raw[o][:].rearrange("p r (m t) -> p m t r", t=PACK)
-            sm = SCALAR_M[o]
-            nc.scalar.copy(out=dst[:, :sm], in_=src[:, :sm])
-            if sm < P:
-                nc.vector.tensor_copy(out=dst[:, sm:], in_=src[:, sm:])
-            if o == 0:
-                nc.vector.tensor_copy(es[:], es_tab[:].indirect(txt_t[:]))
-            codes = keep.tile([P, H], U32, name=f"w_codes{o}", tag=f"wc{o}", align_bytes=64)
-            scales = keep.tile([P, H], U8, name=f"w_scales{o}", align_bytes=64)
-            if o == 1:
-                x1_first = keep.tile([P, P], U32, name="x1_first", align_bytes=64)
-                nc.vector.tensor_copy(x1_first[:], xw_tab[1][:].bitcast(U32).indirect(offs_t[:, 0:LCOL]))
-            pieces = 1 if o == 0 else 4
-            for i in range(pieces):
-                n = H // pieces
-                nc.vector.quantize_mx(out=codes[:, i * n : (i + 1) * n].bitcast(FP8X4), scales=scales[:, i * n : (i + 1) * n], in_=w_bf[:, i * n * PACK : (i + 1) * n * PACK])
-            w_codes.append(codes)
-            w_scales.append(scales)
+            split = SCALAR_GROUPS[o]
+            nc.scalar.copy(out=dst[:, :split], in_=src[:, :split])
+            nc.vector.tensor_copy(out=dst[:, split:], in_=src[:, split:])
+            return w_bf
 
-        ew_tab = keep.tile([P, W], I32, name="ew_tab", tag="xw0", align_bytes=64)
+        def quantise_w(o, w_bf, pieces):
+            codes = keep.tile([P, H], U32, name=f"w_codes{o}", tag=f"w_codes{o}", align_bytes=ALIGN)
+            scales = keep.tile([P, H], U8, name=f"w_scales{o}", align_bytes=ALIGN)
+            n = H // pieces
+            for i in range(pieces):
+                nc.vector.quantize_mx(
+                    out=codes[:, i * n : (i + 1) * n].bitcast(FP8X4),
+                    scales=scales[:, i * n : (i + 1) * n],
+                    in_=w_bf[:, i * n * PACK : (i + 1) * n * PACK],
+                )
+            return codes, scales
+
+        def gather_x1(dst, c):
+            per_chunk = P // LIST
+            nc.vector.tensor_copy(dst, xw_tab[1][:].bitcast(U32).indirect(offs_t[:, c * per_chunk : (c + 1) * per_chunk]))
+
+        w_bf0 = round_w(0)
+        es = keep.tile([P, V], U8, name="es", align_bytes=ALIGN)
+        nc.vector.tensor_copy(es[:], es_tab[:].indirect(txt_t[:]))
+        w_mx = [quantise_w(0, w_bf0, 1)]
+
+        w_bf1 = round_w(1)
+        x1_first = keep.tile([P, P], U32, name="x1_first", align_bytes=ALIGN)
+        gather_x1(x1_first[:], 0)
+        w_mx.append(quantise_w(1, w_bf1, PACK))
+
+        ew_tab = keep.tile([P, W], I32, name="ew_tab", tag="words0", align_bytes=ALIGN)
         nc.sync.dma_start(out=ew_tab[:], in_=e_words[0].rearrange("p n t -> p (n t)").bitcast(I32))
-        lab_pairs = []
-        for half in range(2):
-            pair = keep.tile([P, 2, V], F32, name=f"lab{half}", tag=f"big{half}", align_bytes=64)
-            for i in range(2):
-                c = 2 * half + i
+        lab_t = []
+        for half in range(CHUNKS // PAIR):
+            pair = keep.tile([P, PAIR, V], F32, name=f"lab{half}", tag=f"floats{half}", align_bytes=ALIGN)
+            for i in range(PAIR):
+                c = PAIR * half + i
                 nc.sync.dma_start(out=pair[:, i, :], in_=lab[c * P : (c + 1) * P, :])
-            lab_pairs.append(pair)
+                lab_t.append(pair[:, i, :])
 
         x1 = [x1_first[:]]
-        x1_rest = keep.tile([P, S - P], U32, name="x1_rest", tag="wbf1", align_bytes=64)
+        x1_rest = keep.tile([P, S - P], U32, name="x1_rest", tag="w_bf1", align_bytes=ALIGN)
         for c in range(1, CHUNKS):
-            g = x1_rest[:, (c - 1) * P : c * P]
-            nc.vector.tensor_copy(g, xw_tab[1][:].bitcast(U32).indirect(offs_t[:, c * LCOL : (c + 1) * LCOL]))
-            x1.append(g)
+            x1.append(x1_rest[:, (c - 1) * P : c * P])
+            gather_x1(x1[c], c)
 
-        ew = keep.tile([P, V], U32, name="ew", align_bytes=64)
+        ew = keep.tile([P, V], U32, name="ew", align_bytes=ALIGN)
         h_acc = [psum.tile([P, PACK, P], F32, name=f"h_acc{c}") for c in range(CHUNKS)]
+        y_acc = [psum.tile([P, V], F32, name=f"y_acc{c}") for c in range(CHUNKS)]
 
         def project(c, t, o):
-            cols = slice(c * P, (c + 1) * P)
-            wcols = slice(t * P, (t + 1) * P)
-            rhs = x0[:, cols] if o == 0 else x1[c]
+            images = slice(c * P, (c + 1) * P)
+            places = slice(t * P, (t + 1) * P)
+            codes, scales = w_mx[o]
             nc.tensor.matmul_mx(
                 out=h_acc[c][:, t, :],
-                lhsT=w_codes[o][:, wcols].bitcast(FP8X4),
-                lhsT_scale=w_scales[o][:, wcols],
-                rhs=rhs.bitcast(FP8X4),
-                rhs_scale=xs[4 * o : P, cols],
+                lhsT=codes[:, places].bitcast(FP8X4),
+                lhsT_scale=scales[:, places],
+                rhs=(x0[:, images] if o == 0 else x1[c]).bitcast(FP8X4),
+                rhs_scale=xs[ROWS * o : P, images],
                 start=(o == 0),
                 stop=(o == PASSES - 1),
             )
 
-        y_acc = [psum.tile([P, V], F32, name=f"y{c}") for c in range(CHUNKS)]
-        for i in range(3):
-            nc.tensor.matmul_mx(
-                out=y_acc[CHUNKS - 1 - i][:],
-                lhsT=w_codes[0][:, 0:P].bitcast(FP8X4),
-                lhsT_scale=w_scales[0][:, 0:P],
-                rhs=x0[:].bitcast(FP8X4),
-                rhs_scale=xs[:],
-                start=True,
-                stop=True,
-            )
+        def round_h(c):
+            h_bf = keep.tile([P, P, PACK], BF16, name=f"h_bf{c}", align_bytes=ALIGN)
+            nc.scalar.copy(out=h_bf[:], in_=h_acc[c][:].rearrange("p t n -> p n t"))
+            return h_bf
+
         for c in range(CHUNKS):
             project(c, 0, 0)
-        h_codes, h_scales, shifts = [], [], []
+        h_scales = []
         for c in range(CHUNKS):
-            acc = h_acc[c]
-            for t in range(PACK):
+            project(c, 0, 1)
+            for t in range(1, PACK):
                 for o in range(PASSES):
-                    if (t, o) != (0, 0):
-                        project(c, t, o)
-            h_bf = keep.tile([P, P, PACK], BF16, name=f"h_bf{c}", tag=f"hbf{c}", align_bytes=64)
-            nc.scalar.copy(out=h_bf[:], in_=acc[:].rearrange("p t n -> p n t"))
+                    project(c, t, o)
+            h_bf = round_h(c)
             if c == 0:
                 nc.vector.tensor_copy(ew[:], ew_tab[:].bitcast(U32).indirect(txt_t[:]))
-                all_codes = keep.tile([P, S], U32, name="all_codes", tag="xw0", align_bytes=64)
-            codes = all_codes[:, c * P : (c + 1) * P]
-            scales = keep.tile([P, P], U8, name=f"h_scales{c}", align_bytes=64)
-            nc.vector.quantize_mx(out=codes.bitcast(FP8X4), scales=scales[:], in_=h_bf[:].rearrange("p n t -> p (n t)"))
-            h_codes.append(codes)
+                h_codes = keep.tile([P, S], U32, name="h_codes", tag="words0", align_bytes=ALIGN)
+            scales = keep.tile([P, P], U8, name=f"h_scales{c}", align_bytes=ALIGN)
+            nc.vector.quantize_mx(
+                out=h_codes[:, c * P : (c + 1) * P].bitcast(FP8X4),
+                scales=scales[:],
+                in_=h_bf[:].rearrange("p n t -> p (n t)"),
+            )
             h_scales.append(scales)
 
-        res = keep.tile([P, CHUNKS, V], F32, name="res", align_bytes=64)
+        res = keep.tile([P, CHUNKS, V], F32, name="res", align_bytes=ALIGN)
         for c in range(CHUNKS):
-            if c < 2:
-                shift = keep.tile([P, 2, V], F32, name=f"shift{c}", align_bytes=64)
-                nc.vector.tensor_scalar(out=shift[:], in0=lab_pairs[c][:], scalar1=0.75, scalar2=None, op0=ALU.mult)
-                shifts.extend([shift[:, 0, :], shift[:, 1, :]])
-            y = y_acc[c]
+            images = slice(c * P, (c + 1) * P)
+            shift = keep.tile([P, V], F32, name=f"shift{c}", align_bytes=ALIGN)
+            nc.gpsimd.tensor_scalar(out=shift[:], in0=lab_t[c], scalar1=0.75, scalar2=0.0, op0=ALU.mult, op1=ALU.add)
             nc.tensor.matmul_mx(
-                out=y[:],
-                lhsT=h_codes[c].bitcast(FP8X4),
+                out=y_acc[c][:],
+                lhsT=h_codes[:, images].bitcast(FP8X4),
                 lhsT_scale=h_scales[c][:],
                 rhs=ew[:].bitcast(FP8X4),
                 rhs_scale=es[:],
                 start=True,
                 stop=True,
             )
-            th = keep.tile([P, V], F32, name=f"th{c}", align_bytes=64)
-            nc.scalar.activation(out=th[:], in_=y[:], func=ACT.Tanh, bias=-0.25, scale=0.75)
-            nc.vector.scalar_tensor_tensor(out=res[:, c, :], in0=th[:], scalar=0.75, in1=shifts[c], op0=ALU.mult, op1=ALU.subtract)
-            nc.sync.dma_start(out=out[c * P : (c + 1) * P, :], in_=res[:, c, :])
+            th = keep.tile([P, V], F32, name=f"th{c}", align_bytes=ALIGN)
+            nc.scalar.activation(out=th[:], in_=y_acc[c][:], func=ACT.Tanh, bias=-0.25, scale=0.75)
+            parts = LAST_PARTS if c == CHUNKS - 1 else 1
+            for i in range(parts):
+                texts = slice(i * V // parts, (i + 1) * V // parts)
+                nc.vector.scalar_tensor_tensor(
+                    out=res[:, c, texts], in0=th[:, texts], scalar=0.75, in1=shift[:, texts], op0=ALU.mult, op1=ALU.subtract
+                )
+                nc.sync.dma_start(out=out[images, texts], in_=res[:, c, texts])

@@ -24,59 +24,80 @@ LIST = 16
 ALIGN = 64
 PASSES = K // (P * PACK)
 CHUNKS = S // P
-PAIR = 2
-SCALAR_GROUPS = (96, 64)
+SCALAR_GROUPS = (92, 64)
 LAST_PARTS = 2
+EARLY = 1
+X1_RUNS = (1, 1, 1, 1,)
+E_AT = 0
+WBF_AT = W * 4
+LAB_AT = WBF_AT + 2 * PACK * H * 2
 
 
 def tile_picked_ysiglip_grad_p_kernel(tc, x_words, x_scales, w1, e_words, e_scales, lab, offs, txt, out):
     nc = tc.nc
     with ExitStack() as ctx:
         keep = ctx.enter_context(tc.tile_pool(name="keep", bufs=1))
+        over = ctx.enter_context(tc.tile_pool(name="over", bufs=1))
         psum = ctx.enter_context(tc.psum_pool(name="psum", bufs=1))
 
         offs_t = keep.tile([P, S // LIST], U16, name="offs_t")
         txt_t = keep.tile([P, V // LIST], U16, name="txt_t")
-
         xs_tab = keep.tile([P, T], U8, name="xs_tab", align_bytes=ALIGN)
-        es_tab = keep.tile([P, W], U8, name="es_tab", tag="w_codes0", align_bytes=ALIGN)
+        es_tab = keep.tile([P, W], U8, name="es_tab", align_bytes=ALIGN)
         nc.vector.memset(xs_tab[:].bitcast(I32), 0)
         nc.gpsimd.memset(es_tab[:].bitcast(I32), 0)
 
-        xw_tab = [keep.tile([P, T], I32, name=f"xw_tab{o}", tag=f"words{o}", align_bytes=ALIGN) for o in range(PASSES)]
-        w_raw = [keep.tile([P, PACK, H], F32, name=f"w_raw{o}", tag=f"floats{o}", align_bytes=ALIGN) for o in range(PASSES)]
+        xw_tab = [keep.tile([P, T], I32, name=f"xw_tab{o}", align_bytes=ALIGN) for o in range(PASSES)]
+        w_raw = [keep.tile([P, PACK, H], F32, name=f"w_raw{o}", align_bytes=ALIGN) for o in range(PASSES)]
+        ew_tab = over.tile([P, W], I32, name="ew_tab", align_bytes=ALIGN, offset=E_AT)
 
         def load_w(o):
-            rows = w1[o * P * PACK : (o + 1) * P * PACK, :]
-            nc.sync.dma_start(out=w_raw[o][:], in_=rows.rearrange("(p r) c -> p r c", r=PACK))
+            rows = w1[o * P * PACK : (o + 1) * P * PACK, :].rearrange("(p r) c -> p r c", r=PACK)
+            nc.sync.dma_start(out=w_raw[o][:], in_=rows)
 
         def load_x(o):
             nc.sync.dma_start(out=xw_tab[o][:], in_=x_words[o].rearrange("p n t -> p (n t)").bitcast(I32))
 
-        nc.sync.dma_start(offs_t[:], offs)
+        def load_xs():
+            for q in range(QUADS):
+                nc.sync.dma_start(
+                    out=xs_tab[QUAD * q : QUAD * q + ROWS * PASSES, :].bitcast(I32),
+                    in_=x_scales[:, ROWS * q : ROWS * (q + 1), :].bitcast(I32),
+                )
+
+        def load_es():
+            for r in range(ROWS):
+                nc.sync.dma_start(
+                    out=es_tab[8 + r : P : QUAD, :].bitcast(I32),
+                    in_=e_scales[0, r : ROWS * QUADS : ROWS, :].bitcast(I32),
+                )
+
+        def load_e():
+            nc.sync.dma_start(out=ew_tab[:], in_=e_words[0].rearrange("p n t -> p (n t)").bitcast(I32))
+
         load_x(0)
-        nc.sync.dma_start(txt_t[:], txt)
-        for q in range(QUADS):
-            nc.sync.dma_start(
-                out=xs_tab[QUAD * q : QUAD * q + ROWS * PASSES, :].bitcast(I32),
-                in_=x_scales[:, ROWS * q : ROWS * (q + 1), :].bitcast(I32),
-            )
+        nc.sync.dma_start(offs_t[:], offs)
+        load_xs()
         load_w(0)
-        for r in range(ROWS):
-            nc.sync.dma_start(
-                out=es_tab[r:P:QUAD, :].bitcast(I32),
-                in_=e_scales[0, r : ROWS * QUADS : ROWS, :].bitcast(I32),
-            )
+        nc.sync.dma_start(txt_t[:], txt)
+        load_es()
         load_w(1)
         load_x(1)
+        load_e()
 
-        xs = keep.tile([P, S], U8, name="xs", align_bytes=ALIGN)
-        nc.vector.tensor_copy(xs[:], xs_tab[:].indirect(offs_t[:]))
         x0 = keep.tile([P, S], U32, name="x0", align_bytes=ALIGN)
         nc.vector.tensor_copy(x0[:], xw_tab[0][:].bitcast(U32).indirect(offs_t[:]))
+        xs = keep.tile([P, S], U8, name="xs", align_bytes=ALIGN)
+        nc.vector.tensor_copy(xs[:], xs_tab[:].indirect(offs_t[:]))
+        es = keep.tile([P, V], U8, name="es", align_bytes=ALIGN)
+        nc.vector.tensor_copy(es[:], es_tab[:].indirect(txt_t[:]))
+
+        lab_t = over.tile([P, CHUNKS, V], F32, name="lab_t", align_bytes=ALIGN, offset=LAB_AT)
+        for c in range(CHUNKS):
+            nc.sync.dma_start(out=lab_t[:, c, :], in_=lab[c * P : (c + 1) * P, :])
 
         def round_w(o):
-            w_bf = keep.tile([P, PACK * H], BF16, name=f"w_bf{o}", tag=f"w_bf{o}", align_bytes=ALIGN)
+            w_bf = over.tile([P, PACK * H], BF16, name=f"w_bf{o}", align_bytes=ALIGN, offset=WBF_AT + o * PACK * H * 2)
             dst = w_bf[:].rearrange("p (t m r) -> p m t r", t=PACK, r=PACK)
             src = w_raw[o][:].rearrange("p r (m t) -> p m t r", t=PACK)
             split = SCALAR_GROUPS[o]
@@ -85,7 +106,7 @@ def tile_picked_ysiglip_grad_p_kernel(tc, x_words, x_scales, w1, e_words, e_scal
             return w_bf
 
         def quantise_w(o, w_bf, pieces):
-            codes = keep.tile([P, H], U32, name=f"w_codes{o}", tag=f"w_codes{o}", align_bytes=ALIGN)
+            codes = keep.tile([P, H], U32, name=f"w_codes{o}", align_bytes=ALIGN)
             scales = keep.tile([P, H], U8, name=f"w_scales{o}", align_bytes=ALIGN)
             n = H // pieces
             for i in range(pieces):
@@ -96,35 +117,20 @@ def tile_picked_ysiglip_grad_p_kernel(tc, x_words, x_scales, w1, e_words, e_scal
                 )
             return codes, scales
 
-        def gather_x1(dst, c):
-            per_chunk = P // LIST
-            nc.vector.tensor_copy(dst, xw_tab[1][:].bitcast(U32).indirect(offs_t[:, c * per_chunk : (c + 1) * per_chunk]))
-
         w_bf0 = round_w(0)
-        es = keep.tile([P, V], U8, name="es", align_bytes=ALIGN)
-        nc.vector.tensor_copy(es[:], es_tab[:].indirect(txt_t[:]))
-        w_mx = [quantise_w(0, w_bf0, 1)]
-
+        w_mx = [quantise_w(0, w_bf0, 2)]
         w_bf1 = round_w(1)
-        x1_first = keep.tile([P, P], U32, name="x1_first", align_bytes=ALIGN)
-        gather_x1(x1_first[:], 0)
-        w_mx.append(quantise_w(1, w_bf1, PACK))
+        w_mx.append(quantise_w(1, w_bf1, 2))
 
-        ew_tab = keep.tile([P, W], I32, name="ew_tab", tag="words0", align_bytes=ALIGN)
-        nc.sync.dma_start(out=ew_tab[:], in_=e_words[0].rearrange("p n t -> p (n t)").bitcast(I32))
-        lab_t = []
-        for half in range(CHUNKS // PAIR):
-            pair = keep.tile([P, PAIR, V], F32, name=f"lab{half}", tag=f"floats{half}", align_bytes=ALIGN)
-            for i in range(PAIR):
-                c = PAIR * half + i
-                nc.sync.dma_start(out=pair[:, i, :], in_=lab[c * P : (c + 1) * P, :])
-                lab_t.append(pair[:, i, :])
-
-        x1 = [x1_first[:]]
-        x1_rest = keep.tile([P, S - P], U32, name="x1_rest", tag="w_bf1", align_bytes=ALIGN)
-        for c in range(1, CHUNKS):
-            x1.append(x1_rest[:, (c - 1) * P : c * P])
-            gather_x1(x1[c], c)
+        x1 = []
+        c0 = 0
+        for run in X1_RUNS:
+            piece = keep.tile([P, run * P], U32, name=f"x1_{c0}", align_bytes=ALIGN)
+            per_chunk = P // LIST
+            nc.vector.tensor_copy(piece[:], xw_tab[1][:].bitcast(U32).indirect(offs_t[:, c0 * per_chunk : (c0 + run) * per_chunk]))
+            for i in range(run):
+                x1.append(piece[:, i * P : (i + 1) * P])
+            c0 = c0 + run
 
         ew = keep.tile([P, V], U32, name="ew", align_bytes=ALIGN)
         h_acc = [psum.tile([P, PACK, P], F32, name=f"h_acc{c}") for c in range(CHUNKS)]
@@ -140,55 +146,59 @@ def tile_picked_ysiglip_grad_p_kernel(tc, x_words, x_scales, w1, e_words, e_scal
                 lhsT_scale=scales[:, places],
                 rhs=(x0[:, images] if o == 0 else x1[c]).bitcast(FP8X4),
                 rhs_scale=xs[ROWS * o : P, images],
-                start=(o == 0),
-                stop=(o == PASSES - 1),
+                start=(o == 0 and t == 0),
+                stop=(o == PASSES - 1 and t == PACK - 1),
             )
 
-        def round_h(c):
+        for t in range(PACK):
+            for c in range(CHUNKS):
+                project(c, t, 0)
+        h_mx = []
+        hb = []
+        for c in range(CHUNKS):
+            for t in range(PACK):
+                project(c, t, 1)
             h_bf = keep.tile([P, P, PACK], BF16, name=f"h_bf{c}", align_bytes=ALIGN)
+            hb.append(h_bf)
             nc.scalar.copy(out=h_bf[:], in_=h_acc[c][:].rearrange("p t n -> p n t"))
-            return h_bf
-
-        for c in range(CHUNKS):
-            project(c, 0, 0)
-        h_scales = []
-        for c in range(CHUNKS):
-            project(c, 0, 1)
-            for t in range(1, PACK):
-                for o in range(PASSES):
-                    project(c, t, o)
-            h_bf = round_h(c)
             if c == 0:
                 nc.vector.tensor_copy(ew[:], ew_tab[:].bitcast(U32).indirect(txt_t[:]))
-                h_codes = keep.tile([P, S], U32, name="h_codes", tag="words0", align_bytes=ALIGN)
+            if c < 0:
+                codes = keep.tile([P, P], U32, name=f"h_codes{c}", align_bytes=ALIGN)
+            else:
+                codes = over.tile([P, P], U32, name=f"h_codes{c}", align_bytes=ALIGN, offset=E_AT + c * P * 4)
             scales = keep.tile([P, P], U8, name=f"h_scales{c}", align_bytes=ALIGN)
             nc.vector.quantize_mx(
-                out=h_codes[:, c * P : (c + 1) * P].bitcast(FP8X4),
+                out=codes[:].bitcast(FP8X4),
                 scales=scales[:],
                 in_=h_bf[:].rearrange("p n t -> p (n t)"),
             )
-            h_scales.append(scales)
+            h_mx.append((codes, scales))
 
+        shift = []
+        shift_engines = (nc.vector, nc.vector, nc.vector, nc.vector)
+        for c in range(CHUNKS):
+            scaled = keep.tile([P, V], F32, name=f"shift{c}", align_bytes=ALIGN)
+            shift_engines[c].tensor_scalar(out=scaled[:], in0=lab_t[:, c, :], scalar1=0.75, scalar2=0.0, op0=ALU.mult, op1=ALU.add)
+            shift.append(scaled)
         res = keep.tile([P, CHUNKS, V], F32, name="res", align_bytes=ALIGN)
         for c in range(CHUNKS):
             images = slice(c * P, (c + 1) * P)
-            shift = keep.tile([P, V], F32, name=f"shift{c}", align_bytes=ALIGN)
-            nc.gpsimd.tensor_scalar(out=shift[:], in0=lab_t[c], scalar1=0.75, scalar2=0.0, op0=ALU.mult, op1=ALU.add)
             nc.tensor.matmul_mx(
                 out=y_acc[c][:],
-                lhsT=h_codes[:, images].bitcast(FP8X4),
-                lhsT_scale=h_scales[c][:],
+                lhsT=h_mx[c][0][:].bitcast(FP8X4),
+                lhsT_scale=h_mx[c][1][:],
                 rhs=ew[:].bitcast(FP8X4),
-                rhs_scale=es[:],
+                rhs_scale=es[8:P, :],
                 start=True,
                 stop=True,
             )
             th = keep.tile([P, V], F32, name=f"th{c}", align_bytes=ALIGN)
-            nc.scalar.activation(out=th[:], in_=y_acc[c][:], func=ACT.Tanh, bias=-0.25, scale=0.75)
             parts = LAST_PARTS if c == CHUNKS - 1 else 1
             for i in range(parts):
                 texts = slice(i * V // parts, (i + 1) * V // parts)
+                nc.scalar.activation(out=th[:, texts], in_=y_acc[c][:, texts], func=ACT.Tanh, bias=-0.25, scale=0.75)
                 nc.vector.scalar_tensor_tensor(
-                    out=res[:, c, texts], in0=th[:, texts], scalar=0.75, in1=shift[:, texts], op0=ALU.mult, op1=ALU.subtract
+                    out=res[:, c, texts], in0=th[:, texts], scalar=0.75, in1=shift[c][:, texts], op0=ALU.mult, op1=ALU.subtract
                 )
                 nc.sync.dma_start(out=out[images, texts], in_=res[:, c, texts])

@@ -25,6 +25,7 @@ ALIGN = 64
 PASSES = K // (P * PACK)
 CHUNKS = S // P
 SCALAR_GROUPS = (92, 64)
+LAB_RUNS = ((0, 1), (1, 3), (3, 4))
 LAST_PARTS = 2
 EARLY = 1
 X1_RUNS = (1, 1, 1, 1,)
@@ -92,9 +93,12 @@ def tile_picked_ysiglip_grad_p_kernel(tc, x_words, x_scales, w1, e_words, e_scal
         es = keep.tile([P, V], U8, name="es", align_bytes=ALIGN)
         nc.vector.tensor_copy(es[:], es_tab[:].indirect(txt_t[:]))
 
-        lab_t = over.tile([P, CHUNKS, V], F32, name="lab_t", align_bytes=ALIGN, offset=LAB_AT)
-        for c in range(CHUNKS):
-            nc.sync.dma_start(out=lab_t[:, c, :], in_=lab[c * P : (c + 1) * P, :])
+        lab_rows = lab.rearrange("(c p) v -> p c v", p=P)
+        lab_t = []
+        for c0, c1 in LAB_RUNS:
+            labels = over.tile([P, c1 - c0, V], F32, name=f"lab{c0}", align_bytes=ALIGN, offset=LAB_AT + c0 * V * 4)
+            nc.sync.dma_start(out=labels[:], in_=lab_rows[:, c0:c1, :])
+            lab_t.append(labels)
 
         def round_w(o):
             w_bf = over.tile([P, PACK * H], BF16, name=f"w_bf{o}", align_bytes=ALIGN, offset=WBF_AT + o * PACK * H * 2)
@@ -175,13 +179,10 @@ def tile_picked_ysiglip_grad_p_kernel(tc, x_words, x_scales, w1, e_words, e_scal
             )
             h_mx.append((codes, scales))
 
-        shift = []
-        shift_engines = (nc.vector, nc.vector, nc.vector, nc.vector)
-        for c in range(CHUNKS):
-            scaled = keep.tile([P, V], F32, name=f"shift{c}", align_bytes=ALIGN)
-            shift_engines[c].tensor_scalar(out=scaled[:], in0=lab_t[:, c, :], scalar1=0.75, scalar2=0.0, op0=ALU.mult, op1=ALU.add)
-            shift.append(scaled)
-        res = keep.tile([P, CHUNKS, V], F32, name="res", align_bytes=ALIGN)
+        shift = keep.tile([P, CHUNKS, V], F32, name="shift", align_bytes=ALIGN)
+        for (c0, c1), engine, labels in zip(LAB_RUNS, (nc.gpsimd, nc.vector, nc.vector), lab_t):
+            engine.tensor_scalar(out=shift[:, c0:c1, :], in0=labels[:], scalar1=0.75, scalar2=0.0, op0=ALU.mult, op1=ALU.add)
+        res = [over.tile([P, V], F32, name=f"res{c}", align_bytes=ALIGN, offset=LAB_AT + (1 if c == 0 else CHUNKS + c) * V * 4) for c in range(CHUNKS)]
         for c in range(CHUNKS):
             images = slice(c * P, (c + 1) * P)
             nc.tensor.matmul_mx(
@@ -194,11 +195,11 @@ def tile_picked_ysiglip_grad_p_kernel(tc, x_words, x_scales, w1, e_words, e_scal
                 stop=True,
             )
             th = keep.tile([P, V], F32, name=f"th{c}", align_bytes=ALIGN)
-            parts = LAST_PARTS if c == CHUNKS - 1 else 1
+            parts = LAST_PARTS if c in (0, CHUNKS - 1) else 1
             for i in range(parts):
                 texts = slice(i * V // parts, (i + 1) * V // parts)
                 nc.scalar.activation(out=th[:, texts], in_=y_acc[c][:, texts], func=ACT.Tanh, bias=-0.25, scale=0.75)
                 nc.vector.scalar_tensor_tensor(
-                    out=res[:, c, texts], in0=th[:, texts], scalar=0.75, in1=shift[c][:, texts], op0=ALU.mult, op1=ALU.subtract
+                    out=res[c][:, texts], in0=th[:, texts], scalar=0.75, in1=shift[:, c, texts], op0=ALU.mult, op1=ALU.subtract
                 )
-                nc.sync.dma_start(out=out[images, texts], in_=res[:, c, texts])
+                nc.sync.dma_start(out=out[images, texts], in_=res[c][:, texts])

@@ -137,7 +137,7 @@ def tile_picked_ysiglip_grad_p_kernel(tc, x_words, x_scales, w1, e_words, e_scal
             c0 = c0 + run
 
         ew = keep.tile([P, V], U32, name="ew", align_bytes=ALIGN)
-        h_acc = [psum.tile([P, PACK, P], F32, name=f"h_acc{c}") for c in range(CHUNKS)]
+        h_acc = [psum.tile([P, PACK, P], F32, name=f"h_acc{c}", tag=f"h{c}") for c in range(CHUNKS)]
         y_acc = [psum.tile([P, V], F32, name=f"y_acc{c}") for c in range(CHUNKS)]
 
         def project(c, t, o):
@@ -159,47 +159,55 @@ def tile_picked_ysiglip_grad_p_kernel(tc, x_words, x_scales, w1, e_words, e_scal
                 project(c, t, 0)
         h_mx = []
         hb = []
+        h_all = keep.tile([P, CHUNKS, P, PACK], BF16, name="h_all", align_bytes=ALIGN)
         for c in range(CHUNKS):
             for t in range(PACK):
                 project(c, t, 1)
-            h_bf = keep.tile([P, P, PACK], BF16, name=f"h_bf{c}", align_bytes=ALIGN)
+            h_bf = h_all[:, c, :, :]
             hb.append(h_bf)
-            nc.scalar.copy(out=h_bf[:], in_=h_acc[c][:].rearrange("p t n -> p n t"))
+            nc.scalar.copy(out=h_bf, in_=h_acc[c][:].rearrange("p t n -> p n t"))
             if c == 0:
                 nc.vector.tensor_copy(ew[:], ew_tab[:].bitcast(U32).indirect(txt_t[:]))
-            if c < 0:
-                codes = keep.tile([P, P], U32, name=f"h_codes{c}", align_bytes=ALIGN)
-            else:
-                codes = over.tile([P, P], U32, name=f"h_codes{c}", align_bytes=ALIGN, offset=E_AT + c * P * 4)
-            scales = keep.tile([P, P], U8, name=f"h_scales{c}", align_bytes=ALIGN)
-            nc.vector.quantize_mx(
-                out=codes[:].bitcast(FP8X4),
-                scales=scales[:],
-                in_=h_bf[:].rearrange("p n t -> p (n t)"),
-            )
-            h_mx.append((codes, scales))
-
         shift = keep.tile([P, CHUNKS, V], F32, name="shift", align_bytes=ALIGN)
         for (c0, c1), engine, labels in zip(LAB_RUNS, (nc.gpsimd, nc.vector, nc.vector), lab_t):
             engine.tensor_scalar(out=shift[:, c0:c1, :], in0=labels[:], scalar1=0.75, scalar2=0.0, op0=ALU.mult, op1=ALU.add)
+        for c0, c1 in ((0, 1), (1, 3), (3, 4)):
+            n = c1 - c0
+            codes = over.tile([P, n * P], U32, name=f"h_codes{c0}", align_bytes=ALIGN, offset=E_AT + c0 * P * 4 if c0 < 3 else LAB_AT + 2 * V * 4)
+            scales = keep.tile([P, n * P], U8, name=f"h_scales{c0}", align_bytes=ALIGN)
+            nc.vector.quantize_mx(
+                out=codes[:].bitcast(FP8X4),
+                scales=scales[:],
+                in_=h_all[:, c0:c1, :, :].rearrange("p c n t -> p (c n t)"),
+            )
+            for i in range(n):
+                h_mx.append((codes[:, i * P : (i + 1) * P], scales[:, i * P : (i + 1) * P]))
+
         res = [over.tile([P, V], F32, name=f"res{c}", align_bytes=ALIGN, offset=LAB_AT + (1 if c == 0 else CHUNKS + c) * V * 4) for c in range(CHUNKS)]
+        y_spare = psum.tile([P, V], F32, name="y_spare", tag="h0")
         for c in range(CHUNKS):
             images = slice(c * P, (c + 1) * P)
-            nc.tensor.matmul_mx(
-                out=y_acc[c][:],
-                lhsT=h_mx[c][0][:].bitcast(FP8X4),
-                lhsT_scale=h_mx[c][1][:],
-                rhs=ew[:].bitcast(FP8X4),
-                rhs_scale=es[8:P, :],
-                start=True,
-                stop=True,
-            )
+            products = 2 if c == 0 else 1
+            for i in range(products):
+                texts = slice(i * V // products, (i + 1) * V // products)
+                nc.tensor.matmul_mx(
+                    out=(y_acc[c] if i == 0 else y_spare)[:, texts],
+                    lhsT=h_mx[c][0].bitcast(FP8X4),
+                    lhsT_scale=h_mx[c][1],
+                    rhs=ew[:, texts].bitcast(FP8X4),
+                    rhs_scale=es[8:P, texts],
+                    start=True,
+                    stop=True,
+                )
             th = keep.tile([P, V], F32, name=f"th{c}", align_bytes=ALIGN)
-            parts = LAST_PARTS if c in (0, CHUNKS - 1) else 1
+            parts = LAST_PARTS
             for i in range(parts):
                 texts = slice(i * V // parts, (i + 1) * V // parts)
-                nc.scalar.activation(out=th[:, texts], in_=y_acc[c][:, texts], func=ACT.Tanh, bias=-0.25, scale=0.75)
+                nc.scalar.activation(out=th[:, texts], in_=(y_spare if c == 0 and i == 1 else y_acc[c])[:, texts], func=ACT.Tanh, bias=-0.25, scale=0.75)
                 nc.vector.scalar_tensor_tensor(
                     out=res[c][:, texts], in0=th[:, texts], scalar=0.75, in1=shift[:, c, texts], op0=ALU.mult, op1=ALU.subtract
                 )
-                nc.sync.dma_start(out=out[images, texts], in_=res[c][:, texts])
+                if c in (0, CHUNKS - 1):
+                    nc.sync.dma_start(out=out[images, texts], in_=res[c][:, texts])
+            if c not in (0, CHUNKS - 1):
+                nc.sync.dma_start(out=out[images, :], in_=res[c][:])

@@ -24,25 +24,30 @@ LIST = 16
 ALIGN = 64
 PASSES = K // (P * PACK)
 CHUNKS = S // P
+HALVES = 2
+E_ROW = 8
 SCALAR_GROUPS = (92, 64)
-LAB_RUNS = ((0, 1), (1, 3), (3, 4))
-LAST_PARTS = 2
-EARLY = 1
-X1_RUNS = (1, 1, 1, 1,)
+RUNS = ((0, 1), (1, 3), (3, 4))
+
+CHUNK_WORDS = P * 4
+CHUNK_FLOATS = V * 4
+W_BF_BYTES = PACK * H * 2
 E_AT = 0
-WBF_AT = W * 4
-LAB_AT = WBF_AT + 2 * PACK * H * 2
+W_BF_AT = E_AT + W * 4
+LAB_AT = W_BF_AT + PASSES * W_BF_BYTES
+RES_AT = LAB_AT + CHUNKS * CHUNK_FLOATS
 
 
 def tile_picked_ysiglip_grad_p_kernel(tc, x_words, x_scales, w1, e_words, e_scales, lab, offs, txt, out):
     nc = tc.nc
     with ExitStack() as ctx:
         keep = ctx.enter_context(tc.tile_pool(name="keep", bufs=1))
-        over = ctx.enter_context(tc.tile_pool(name="over", bufs=1))
+        placed = ctx.enter_context(tc.tile_pool(name="placed", bufs=1))
         psum = ctx.enter_context(tc.psum_pool(name="psum", bufs=1))
 
         offs_t = keep.tile([P, S // LIST], U16, name="offs_t")
         txt_t = keep.tile([P, V // LIST], U16, name="txt_t")
+
         xs_tab = keep.tile([P, T], U8, name="xs_tab", align_bytes=ALIGN)
         es_tab = keep.tile([P, W], U8, name="es_tab", align_bytes=ALIGN)
         nc.vector.memset(xs_tab[:].bitcast(I32), 0)
@@ -50,7 +55,7 @@ def tile_picked_ysiglip_grad_p_kernel(tc, x_words, x_scales, w1, e_words, e_scal
 
         xw_tab = [keep.tile([P, T], I32, name=f"xw_tab{o}", align_bytes=ALIGN) for o in range(PASSES)]
         w_raw = [keep.tile([P, PACK, H], F32, name=f"w_raw{o}", align_bytes=ALIGN) for o in range(PASSES)]
-        ew_tab = over.tile([P, W], I32, name="ew_tab", align_bytes=ALIGN, offset=E_AT)
+        ew_tab = placed.tile([P, W], I32, name="ew_tab", align_bytes=ALIGN, offset=E_AT)
 
         def load_w(o):
             rows = w1[o * P * PACK : (o + 1) * P * PACK, :].rearrange("(p r) c -> p r c", r=PACK)
@@ -59,32 +64,23 @@ def tile_picked_ysiglip_grad_p_kernel(tc, x_words, x_scales, w1, e_words, e_scal
         def load_x(o):
             nc.sync.dma_start(out=xw_tab[o][:], in_=x_words[o].rearrange("p n t -> p (n t)").bitcast(I32))
 
-        def load_xs():
-            for q in range(QUADS):
-                nc.sync.dma_start(
-                    out=xs_tab[QUAD * q : QUAD * q + ROWS * PASSES, :].bitcast(I32),
-                    in_=x_scales[:, ROWS * q : ROWS * (q + 1), :].bitcast(I32),
-                )
-
-        def load_es():
-            for r in range(ROWS):
-                nc.sync.dma_start(
-                    out=es_tab[8 + r : P : QUAD, :].bitcast(I32),
-                    in_=e_scales[0, r : ROWS * QUADS : ROWS, :].bitcast(I32),
-                )
-
-        def load_e():
-            nc.sync.dma_start(out=ew_tab[:], in_=e_words[0].rearrange("p n t -> p (n t)").bitcast(I32))
-
         load_x(0)
         nc.sync.dma_start(offs_t[:], offs)
-        load_xs()
+        for q in range(QUADS):
+            nc.sync.dma_start(
+                out=xs_tab[QUAD * q : QUAD * q + ROWS * PASSES, :].bitcast(I32),
+                in_=x_scales[:, ROWS * q : ROWS * (q + 1), :].bitcast(I32),
+            )
         load_w(0)
         nc.sync.dma_start(txt_t[:], txt)
-        load_es()
+        for r in range(ROWS):
+            nc.sync.dma_start(
+                out=es_tab[E_ROW + r : P : QUAD, :].bitcast(I32),
+                in_=e_scales[0, r : ROWS * QUADS : ROWS, :].bitcast(I32),
+            )
         load_w(1)
         load_x(1)
-        load_e()
+        nc.sync.dma_start(out=ew_tab[:], in_=e_words[0].rearrange("p n t -> p (n t)").bitcast(I32))
 
         x0 = keep.tile([P, S], U32, name="x0", align_bytes=ALIGN)
         nc.vector.tensor_copy(x0[:], xw_tab[0][:].bitcast(U32).indirect(offs_t[:]))
@@ -94,26 +90,23 @@ def tile_picked_ysiglip_grad_p_kernel(tc, x_words, x_scales, w1, e_words, e_scal
         nc.vector.tensor_copy(es[:], es_tab[:].indirect(txt_t[:]))
 
         lab_rows = lab.rearrange("(c p) v -> p c v", p=P)
-        lab_t = []
-        for c0, c1 in LAB_RUNS:
-            labels = over.tile([P, c1 - c0, V], F32, name=f"lab{c0}", align_bytes=ALIGN, offset=LAB_AT + c0 * V * 4)
+        lab_runs = []
+        for c0, c1 in RUNS:
+            labels = placed.tile([P, c1 - c0, V], F32, name=f"lab{c0}", align_bytes=ALIGN, offset=LAB_AT + c0 * CHUNK_FLOATS)
             nc.sync.dma_start(out=labels[:], in_=lab_rows[:, c0:c1, :])
-            lab_t.append(labels)
+            lab_runs.append(labels)
 
-        def round_w(o):
-            w_bf = over.tile([P, PACK * H], BF16, name=f"w_bf{o}", align_bytes=ALIGN, offset=WBF_AT + o * PACK * H * 2)
-            dst = w_bf[:].rearrange("p (t m r) -> p m t r", t=PACK, r=PACK)
-            src = w_raw[o][:].rearrange("p r (m t) -> p m t r", t=PACK)
+        def quantise_w(o):
+            w_bf = placed.tile([P, PACK * H], BF16, name=f"w_bf{o}", align_bytes=ALIGN, offset=W_BF_AT + o * W_BF_BYTES)
+            dst = w_bf[:].rearrange("p (t m r) -> p m r t", t=PACK, r=PACK)
+            src = w_raw[o][:].rearrange("p r (m t) -> p m r t", t=PACK)
             split = SCALAR_GROUPS[o]
             nc.scalar.copy(out=dst[:, :split], in_=src[:, :split])
             nc.vector.tensor_copy(out=dst[:, split:], in_=src[:, split:])
-            return w_bf
-
-        def quantise_w(o, w_bf, pieces):
             codes = keep.tile([P, H], U32, name=f"w_codes{o}", align_bytes=ALIGN)
             scales = keep.tile([P, H], U8, name=f"w_scales{o}", align_bytes=ALIGN)
-            n = H // pieces
-            for i in range(pieces):
+            n = H // HALVES
+            for i in range(HALVES):
                 nc.vector.quantize_mx(
                     out=codes[:, i * n : (i + 1) * n].bitcast(FP8X4),
                     scales=scales[:, i * n : (i + 1) * n],
@@ -121,20 +114,14 @@ def tile_picked_ysiglip_grad_p_kernel(tc, x_words, x_scales, w1, e_words, e_scal
                 )
             return codes, scales
 
-        w_bf0 = round_w(0)
-        w_mx = [quantise_w(0, w_bf0, 2)]
-        w_bf1 = round_w(1)
-        w_mx.append(quantise_w(1, w_bf1, 2))
+        w_mx = [quantise_w(o) for o in range(PASSES)]
 
         x1 = []
-        c0 = 0
-        for run in X1_RUNS:
-            piece = keep.tile([P, run * P], U32, name=f"x1_{c0}", align_bytes=ALIGN)
-            per_chunk = P // LIST
-            nc.vector.tensor_copy(piece[:], xw_tab[1][:].bitcast(U32).indirect(offs_t[:, c0 * per_chunk : (c0 + run) * per_chunk]))
-            for i in range(run):
-                x1.append(piece[:, i * P : (i + 1) * P])
-            c0 = c0 + run
+        for c in range(CHUNKS):
+            words = keep.tile([P, P], U32, name=f"x1_{c}", align_bytes=ALIGN)
+            entries = offs_t[:, c * P // LIST : (c + 1) * P // LIST]
+            nc.vector.tensor_copy(words[:], xw_tab[1][:].bitcast(U32).indirect(entries))
+            x1.append(words)
 
         ew = keep.tile([P, V], U32, name="ew", align_bytes=ALIGN)
         h_acc = [psum.tile([P, PACK, P], F32, name=f"h_acc{c}", tag=f"h{c}") for c in range(CHUNKS)]
@@ -148,7 +135,7 @@ def tile_picked_ysiglip_grad_p_kernel(tc, x_words, x_scales, w1, e_words, e_scal
                 out=h_acc[c][:, t, :],
                 lhsT=codes[:, places].bitcast(FP8X4),
                 lhsT_scale=scales[:, places],
-                rhs=(x0[:, images] if o == 0 else x1[c]).bitcast(FP8X4),
+                rhs=(x0[:, images] if o == 0 else x1[c][:]).bitcast(FP8X4),
                 rhs_scale=xs[ROWS * o : P, images],
                 start=(o == 0 and t == 0),
                 stop=(o == PASSES - 1 and t == PACK - 1),
@@ -157,57 +144,61 @@ def tile_picked_ysiglip_grad_p_kernel(tc, x_words, x_scales, w1, e_words, e_scal
         for t in range(PACK):
             for c in range(CHUNKS):
                 project(c, t, 0)
-        h_mx = []
-        hb = []
-        h_all = keep.tile([P, CHUNKS, P, PACK], BF16, name="h_all", align_bytes=ALIGN)
+        h_bf = keep.tile([P, CHUNKS, P, PACK], BF16, name="h_bf", align_bytes=ALIGN)
         for c in range(CHUNKS):
             for t in range(PACK):
                 project(c, t, 1)
-            h_bf = h_all[:, c, :, :]
-            hb.append(h_bf)
-            nc.scalar.copy(out=h_bf, in_=h_acc[c][:].rearrange("p t n -> p n t"))
+            nc.scalar.copy(out=h_bf[:, c, :, :], in_=h_acc[c][:].rearrange("p t n -> p n t"))
             if c == 0:
                 nc.vector.tensor_copy(ew[:], ew_tab[:].bitcast(U32).indirect(txt_t[:]))
+
         shift = keep.tile([P, CHUNKS, V], F32, name="shift", align_bytes=ALIGN)
-        for (c0, c1), engine, labels in zip(LAB_RUNS, (nc.gpsimd, nc.vector, nc.vector), lab_t):
+        for (c0, c1), engine, labels in zip(RUNS, (nc.gpsimd, nc.vector, nc.vector), lab_runs):
             engine.tensor_scalar(out=shift[:, c0:c1, :], in0=labels[:], scalar1=0.75, scalar2=0.0, op0=ALU.mult, op1=ALU.add)
-        for c0, c1 in ((0, 1), (1, 3), (3, 4)):
+
+        h_mx = []
+        for c0, c1 in RUNS:
             n = c1 - c0
-            codes = over.tile([P, n * P], U32, name=f"h_codes{c0}", align_bytes=ALIGN, offset=E_AT + c0 * P * 4 if c0 < 3 else LAB_AT + 2 * V * 4)
+            at = E_AT + c0 * CHUNK_WORDS if c1 < CHUNKS else LAB_AT + (c0 - 1) * CHUNK_FLOATS
+            codes = placed.tile([P, n * P], U32, name=f"h_codes{c0}", align_bytes=ALIGN, offset=at)
             scales = keep.tile([P, n * P], U8, name=f"h_scales{c0}", align_bytes=ALIGN)
             nc.vector.quantize_mx(
                 out=codes[:].bitcast(FP8X4),
                 scales=scales[:],
-                in_=h_all[:, c0:c1, :, :].rearrange("p c n t -> p (c n t)"),
+                in_=h_bf[:, c0:c1, :, :].rearrange("p c n t -> p (c n t)"),
             )
             for i in range(n):
                 h_mx.append((codes[:, i * P : (i + 1) * P], scales[:, i * P : (i + 1) * P]))
 
-        res = [over.tile([P, V], F32, name=f"res{c}", align_bytes=ALIGN, offset=LAB_AT + (1 if c == 0 else CHUNKS + c) * V * 4) for c in range(CHUNKS)]
+        res = [
+            placed.tile([P, V], F32, name=f"res{c}", align_bytes=ALIGN, offset=LAB_AT + CHUNK_FLOATS if c == 0 else RES_AT + c * CHUNK_FLOATS)
+            for c in range(CHUNKS)
+        ]
         y_spare = psum.tile([P, V], F32, name="y_spare", tag="h0")
         for c in range(CHUNKS):
             images = slice(c * P, (c + 1) * P)
-            products = 2 if c == 0 else 1
+            banks = (y_acc[c], y_spare if c == 0 else y_acc[c])
+            products = HALVES if c == 0 else 1
             for i in range(products):
                 texts = slice(i * V // products, (i + 1) * V // products)
                 nc.tensor.matmul_mx(
-                    out=(y_acc[c] if i == 0 else y_spare)[:, texts],
+                    out=banks[i][:, texts],
                     lhsT=h_mx[c][0].bitcast(FP8X4),
                     lhsT_scale=h_mx[c][1],
                     rhs=ew[:, texts].bitcast(FP8X4),
-                    rhs_scale=es[8:P, texts],
+                    rhs_scale=es[E_ROW:P, texts],
                     start=True,
                     stop=True,
                 )
             th = keep.tile([P, V], F32, name=f"th{c}", align_bytes=ALIGN)
-            parts = LAST_PARTS
-            for i in range(parts):
-                texts = slice(i * V // parts, (i + 1) * V // parts)
-                nc.scalar.activation(out=th[:, texts], in_=(y_spare if c == 0 and i == 1 else y_acc[c])[:, texts], func=ACT.Tanh, bias=-0.25, scale=0.75)
+            store_halves = c in (0, CHUNKS - 1)
+            for i in range(HALVES):
+                texts = slice(i * V // HALVES, (i + 1) * V // HALVES)
+                nc.scalar.activation(out=th[:, texts], in_=banks[i][:, texts], func=ACT.Tanh, bias=-0.25, scale=0.75)
                 nc.vector.scalar_tensor_tensor(
                     out=res[c][:, texts], in0=th[:, texts], scalar=0.75, in1=shift[:, c, texts], op0=ALU.mult, op1=ALU.subtract
                 )
-                if c in (0, CHUNKS - 1):
+                if store_halves:
                     nc.sync.dma_start(out=out[images, texts], in_=res[c][:, texts])
-            if c not in (0, CHUNKS - 1):
+            if not store_halves:
                 nc.sync.dma_start(out=out[images, :], in_=res[c][:])

@@ -26,7 +26,7 @@ PASSES = K // (P * PACK)
 CHUNKS = S // P
 HALVES = 2
 E_ROW = 8
-SCALAR_GROUPS = (92, 64)
+SCALAR_GROUPS = (92, 54)
 RUNS = ((0, 1), (1, 3), (3, 4))
 
 CHUNK_WORDS = P * 4
@@ -35,7 +35,8 @@ W_BF_BYTES = PACK * H * 2
 E_AT = 0
 W_BF_AT = E_AT + W * 4
 LAB_AT = W_BF_AT + PASSES * W_BF_BYTES
-RES_AT = LAB_AT + CHUNKS * CHUNK_FLOATS
+W1_AT = LAB_AT + CHUNKS * CHUNK_FLOATS
+RES_AT = W1_AT + PACK * H * 4
 
 
 def tile_picked_ysiglip_grad_p_kernel(tc, x_words, x_scales, w1, e_words, e_scales, lab, offs, txt, out):
@@ -54,7 +55,10 @@ def tile_picked_ysiglip_grad_p_kernel(tc, x_words, x_scales, w1, e_words, e_scal
         nc.gpsimd.memset(es_tab[:].bitcast(I32), 0)
 
         xw_tab = [keep.tile([P, T], I32, name=f"xw_tab{o}", align_bytes=ALIGN) for o in range(PASSES)]
-        w_raw = [keep.tile([P, PACK, H], F32, name=f"w_raw{o}", align_bytes=ALIGN) for o in range(PASSES)]
+        w_raw = [
+            keep.tile([P, PACK, H], F32, name="w_raw0", align_bytes=ALIGN),
+            placed.tile([P, PACK, H], F32, name="w_raw1", align_bytes=ALIGN, offset=W1_AT),
+        ]
         ew_tab = placed.tile([P, W], I32, name="ew_tab", align_bytes=ALIGN, offset=E_AT)
 
         def load_w(o):
@@ -106,6 +110,8 @@ def tile_picked_ysiglip_grad_p_kernel(tc, x_words, x_scales, w1, e_words, e_scal
             codes = keep.tile([P, H], U32, name=f"w_codes{o}", align_bytes=ALIGN)
             scales = keep.tile([P, H], U8, name=f"w_scales{o}", align_bytes=ALIGN)
             n = H // HALVES
+            if o == PASSES - 1:
+                gather_x1(0)
             for i in range(HALVES):
                 nc.vector.quantize_mx(
                     out=codes[:, i * n : (i + 1) * n].bitcast(FP8X4),
@@ -114,14 +120,18 @@ def tile_picked_ysiglip_grad_p_kernel(tc, x_words, x_scales, w1, e_words, e_scal
                 )
             return codes, scales
 
-        w_mx = [quantise_w(o) for o in range(PASSES)]
 
-        x1 = []
-        for c in range(CHUNKS):
-            words = keep.tile([P, P], U32, name=f"x1_{c}", align_bytes=ALIGN)
+        x1_first = keep.tile([P, P], U32, name="x1_first", align_bytes=ALIGN)
+        x1_rest = placed.tile([P, S - P], U32, name="x1_rest", align_bytes=ALIGN, offset=W1_AT)
+        x1 = [x1_first[:]] + [x1_rest[:, c * P : (c + 1) * P] for c in range(CHUNKS - 1)]
+
+        def gather_x1(c):
             entries = offs_t[:, c * P // LIST : (c + 1) * P // LIST]
-            nc.vector.tensor_copy(words[:], xw_tab[1][:].bitcast(U32).indirect(entries))
-            x1.append(words)
+            nc.vector.tensor_copy(x1[c], xw_tab[1][:].bitcast(U32).indirect(entries))
+
+        w_mx = [quantise_w(o) for o in range(PASSES)]
+        for c in range(1, CHUNKS):
+            gather_x1(c)
 
         ew = keep.tile([P, V], U32, name="ew", align_bytes=ALIGN)
         h_acc = [psum.tile([P, PACK, P], F32, name=f"h_acc{c}", tag=f"h{c}") for c in range(CHUNKS)]
@@ -135,7 +145,7 @@ def tile_picked_ysiglip_grad_p_kernel(tc, x_words, x_scales, w1, e_words, e_scal
                 out=h_acc[c][:, t, :],
                 lhsT=codes[:, places].bitcast(FP8X4),
                 lhsT_scale=scales[:, places],
-                rhs=(x0[:, images] if o == 0 else x1[c][:]).bitcast(FP8X4),
+                rhs=(x0[:, images] if o == 0 else x1[c]).bitcast(FP8X4),
                 rhs_scale=xs[ROWS * o : P, images],
                 start=(o == 0 and t == 0),
                 stop=(o == PASSES - 1 and t == PACK - 1),

@@ -137,7 +137,7 @@ def tile_picked_ysiglip_grad_p_kernel(tc, x_words, x_scales, w1, e_words, e_scal
         h_acc = [psum.tile([P, PACK, P], F32, name=f"h_acc{c}", tag=f"h{c}") for c in range(CHUNKS)]
         y_acc = [psum.tile([P, V], F32, name=f"y_acc{c}") for c in range(CHUNKS)]
 
-        def project(c, t, o):
+        def project(c, t, o, last):
             images = slice(c * P, (c + 1) * P)
             places = slice(t * P, (t + 1) * P)
             codes, scales = w_mx[o]
@@ -148,16 +148,19 @@ def tile_picked_ysiglip_grad_p_kernel(tc, x_words, x_scales, w1, e_words, e_scal
                 rhs=(x0[:, images] if o == 0 else x1[c]).bitcast(FP8X4),
                 rhs_scale=xs[ROWS * o : P, images],
                 start=(o == 0 and t == 0),
-                stop=(o == PASSES - 1 and t == PACK - 1),
+                stop=last,
             )
 
+        late = [(c, t) for c in range(1, CHUNKS - 1) for t in range(PACK // HALVES, PACK)]
         for t in range(PACK):
             for c in range(CHUNKS):
-                project(c, t, 0)
+                if (c, t) not in late:
+                    project(c, t, 0, last=False)
         h_bf = keep.tile([P, CHUNKS, P, PACK], BF16, name="h_bf", align_bytes=ALIGN)
         for c in range(CHUNKS):
-            for t in range(PACK):
-                project(c, t, 1)
+            passes = [(t, 1) for t in range(PACK)] + [(t, 0) for t in range(PACK) if (c, t) in late]
+            for t, o in passes:
+                project(c, t, o, last=(t, o) == passes[-1])
             nc.scalar.copy(out=h_bf[:, c, :, :], in_=h_acc[c][:].rearrange("p t n -> p n t"))
             if c == 0:
                 nc.vector.tensor_copy(ew[:], ew_tab[:].bitcast(U32).indirect(txt_t[:]))

@@ -26,7 +26,7 @@ PASSES = K // (P * PACK)
 CHUNKS = S // P
 HALVES = 2
 E_ROW = 8
-SCALAR_GROUPS = (92, 54)
+SCALAR_GROUPS = (92, 46)
 RUNS = ((0, 1), (1, 3), (3, 4))
 
 CHUNK_WORDS = P * 4
@@ -172,7 +172,7 @@ def tile_picked_ysiglip_grad_p_kernel(tc, x_words, x_scales, w1, e_words, e_scal
         h_mx = []
         for c0, c1 in RUNS:
             n = c1 - c0
-            at = E_AT + c0 * CHUNK_WORDS if c1 < CHUNKS else LAB_AT + (c0 - 1) * CHUNK_FLOATS
+            at = LAB_AT + c0 * CHUNK_WORDS if c1 < CHUNKS else LAB_AT + (c0 - 1) * CHUNK_FLOATS
             codes = placed.tile([P, n * P], U32, name=f"h_codes{c0}", align_bytes=ALIGN, offset=at)
             scales = keep.tile([P, n * P], U8, name=f"h_scales{c0}", align_bytes=ALIGN)
             nc.vector.quantize_mx(

@@ -21,7 +21,7 @@ QUAD = 32
 QUADS = P // QUAD
 ROWS = 4
 LIST = 16
-ALIGN = 64
+ALIGN = 256
 PASSES = K // (P * PACK)
 CHUNKS = S // P
 HALVES = 2

from contextlib import ExitStack

import concourse.mybir as mybir

K, T, S, H, V, W = 1024, 1024, 512, 512, 512, 2048
FLOPS = 2 * K * H * S + 2 * H * S * V

F32 = mybir.dt.float32
BF16 = mybir.dt.bfloat16
I32 = mybir.dt.int32
U32 = mybir.dt.uint32
U16 = mybir.dt.uint16
U8 = mybir.dt.uint8
FP8X4 = mybir.dt.float8_e4m3fn_x4
ALU = mybir.AluOpType
ACT = mybir.ActivationFunctionType

P = 128
PACK = 4
QUAD = 32
QUADS = P // QUAD
ROWS = 4
LIST = 16
ALIGN = 256
PASSES = K // (P * PACK)
CHUNKS = S // P
HALVES = 2
E_ROW = 8
SCALAR_GROUPS = (92, 46)
RUNS = ((0, 1), (1, 3), (3, 4))

CHUNK_WORDS = P * 4
CHUNK_FLOATS = V * 4
W_BF_BYTES = PACK * H * 2
E_AT = 0
W_BF_AT = E_AT + W * 4
LAB_AT = W_BF_AT + PASSES * W_BF_BYTES
W1_AT = LAB_AT + CHUNKS * CHUNK_FLOATS
RES_AT = W1_AT + PACK * H * 4


def tile_picked_ysiglip_grad_p_kernel(tc, x_words, x_scales, w1, e_words, e_scales, lab, offs, txt, out):
    nc = tc.nc
    with ExitStack() as ctx:
        keep = ctx.enter_context(tc.tile_pool(name="keep", bufs=1))
        placed = ctx.enter_context(tc.tile_pool(name="placed", bufs=1))
        psum = ctx.enter_context(tc.psum_pool(name="psum", bufs=1))

        offs_t = keep.tile([P, S // LIST], U16, name="offs_t")
        txt_t = keep.tile([P, V // LIST], U16, name="txt_t")

        xs_tab = keep.tile([P, T], U8, name="xs_tab", align_bytes=ALIGN)
        es_tab = keep.tile([P, W], U8, name="es_tab", align_bytes=ALIGN)
        nc.vector.memset(xs_tab[:].bitcast(I32), 0)
        nc.gpsimd.memset(es_tab[:].bitcast(I32), 0)

        xw_tab = [keep.tile([P, T], I32, name=f"xw_tab{o}", align_bytes=ALIGN) for o in range(PASSES)]
        w_raw = [
            keep.tile([P, PACK, H], F32, name="w_raw0", align_bytes=ALIGN),
            placed.tile([P, PACK, H], F32, name="w_raw1", align_bytes=ALIGN, offset=W1_AT),
        ]
        ew_tab = placed.tile([P, W], I32, name="ew_tab", align_bytes=ALIGN, offset=E_AT)

        def load_w(o):
            rows = w1[o * P * PACK : (o + 1) * P * PACK, :].rearrange("(p r) c -> p r c", r=PACK)
            nc.sync.dma_start(out=w_raw[o][:], in_=rows)

        def load_x(o):
            nc.sync.dma_start(out=xw_tab[o][:], in_=x_words[o].rearrange("p n t -> p (n t)").bitcast(I32))

        load_x(0)
        nc.sync.dma_start(offs_t[:], offs)
        for q in range(QUADS):
            nc.sync.dma_start(
                out=xs_tab[QUAD * q : QUAD * q + ROWS * PASSES, :].bitcast(I32),
                in_=x_scales[:, ROWS * q : ROWS * (q + 1), :].bitcast(I32),
            )
        load_w(0)
        nc.sync.dma_start(txt_t[:], txt)
        for r in range(ROWS):
            nc.sync.dma_start(
                out=es_tab[E_ROW + r : P : QUAD, :].bitcast(I32),
                in_=e_scales[0, r : ROWS * QUADS : ROWS, :].bitcast(I32),
            )
        load_w(1)
        load_x(1)
        nc.sync.dma_start(out=ew_tab[:], in_=e_words[0].rearrange("p n t -> p (n t)").bitcast(I32))

        x0 = keep.tile([P, S], U32, name="x0", align_bytes=ALIGN)
        nc.vector.tensor_copy(x0[:], xw_tab[0][:].bitcast(U32).indirect(offs_t[:]))
        xs = keep.tile([P, S], U8, name="xs", align_bytes=ALIGN)
        nc.vector.tensor_copy(xs[:], xs_tab[:].indirect(offs_t[:]))
        es = keep.tile([P, V], U8, name="es", align_bytes=ALIGN)
        nc.vector.tensor_copy(es[:], es_tab[:].indirect(txt_t[:]))

        lab_rows = lab.rearrange("(c p) v -> p c v", p=P)
        lab_runs = []
        for c0, c1 in RUNS:
            labels = placed.tile([P, c1 - c0, V], F32, name=f"lab{c0}", align_bytes=ALIGN, offset=LAB_AT + c0 * CHUNK_FLOATS)
            nc.sync.dma_start(out=labels[:], in_=lab_rows[:, c0:c1, :])
            lab_runs.append(labels)

        def quantise_w(o):
            w_bf = placed.tile([P, PACK * H], BF16, name=f"w_bf{o}", align_bytes=ALIGN, offset=W_BF_AT + o * W_BF_BYTES)
            dst = w_bf[:].rearrange("p (t m r) -> p m r t", t=PACK, r=PACK)
            src = w_raw[o][:].rearrange("p r (m t) -> p m r t", t=PACK)
            split = SCALAR_GROUPS[o]
            nc.scalar.copy(out=dst[:, :split], in_=src[:, :split])
            nc.vector.tensor_copy(out=dst[:, split:], in_=src[:, split:])
            codes = keep.tile([P, H], U32, name=f"w_codes{o}", align_bytes=ALIGN)
            scales = keep.tile([P, H], U8, name=f"w_scales{o}", align_bytes=ALIGN)
            n = H // HALVES
            if o == PASSES - 1:
                gather_x1(0)
            for i in range(HALVES):
                nc.vector.quantize_mx(
                    out=codes[:, i * n : (i + 1) * n].bitcast(FP8X4),
                    scales=scales[:, i * n : (i + 1) * n],
                    in_=w_bf[:, i * n * PACK : (i + 1) * n * PACK],
                )
            return codes, scales


        x1_first = keep.tile([P, P], U32, name="x1_first", align_bytes=ALIGN)
        x1_rest = placed.tile([P, S - P], U32, name="x1_rest", align_bytes=ALIGN, offset=W1_AT)
        x1 = [x1_first[:]] + [x1_rest[:, c * P : (c + 1) * P] for c in range(CHUNKS - 1)]

        def gather_x1(c):
            entries = offs_t[:, c * P // LIST : (c + 1) * P // LIST]
            nc.vector.tensor_copy(x1[c], xw_tab[1][:].bitcast(U32).indirect(entries))

        w_mx = [quantise_w(o) for o in range(PASSES)]
        for c in range(1, CHUNKS):
            gather_x1(c)

        ew = keep.tile([P, V], U32, name="ew", align_bytes=ALIGN)
        h_acc = [psum.tile([P, PACK, P], F32, name=f"h_acc{c}", tag=f"h{c}") for c in range(CHUNKS)]
        y_acc = [psum.tile([P, V], F32, name=f"y_acc{c}") for c in range(CHUNKS)]

        def project(c, t, o, last):
            images = slice(c * P, (c + 1) * P)
            places = slice(t * P, (t + 1) * P)
            codes, scales = w_mx[o]
            nc.tensor.matmul_mx(
                out=h_acc[c][:, t, :],
                lhsT=codes[:, places].bitcast(FP8X4),
                lhsT_scale=scales[:, places],
                rhs=(x0[:, images] if o == 0 else x1[c]).bitcast(FP8X4),
                rhs_scale=xs[ROWS * o : P, images],
                start=(o == 0 and t == 0),
                stop=last,
            )

        late = [(c, t) for c in range(1, CHUNKS - 1) for t in range(PACK // HALVES, PACK)]
        for t in range(PACK):
            for c in range(CHUNKS):
                if (c, t) not in late:
                    project(c, t, 0, last=False)
        h_bf = keep.tile([P, CHUNKS, P, PACK], BF16, name="h_bf", align_bytes=ALIGN)
        for c in range(CHUNKS):
            passes = [(t, 1) for t in range(PACK)] + [(t, 0) for t in range(PACK) if (c, t) in late]
            for t, o in passes:
                project(c, t, o, last=(t, o) == passes[-1])
            nc.scalar.copy(out=h_bf[:, c, :, :], in_=h_acc[c][:].rearrange("p t n -> p n t"))
            if c == 0:
                nc.vector.tensor_copy(ew[:], ew_tab[:].bitcast(U32).indirect(txt_t[:]))

        shift = keep.tile([P, CHUNKS, V], F32, name="shift", align_bytes=ALIGN)
        for (c0, c1), engine, labels in zip(RUNS, (nc.gpsimd, nc.vector, nc.vector), lab_runs):
            engine.tensor_scalar(out=shift[:, c0:c1, :], in0=labels[:], scalar1=0.75, scalar2=0.0, op0=ALU.mult, op1=ALU.add)

        h_mx = []
        for c0, c1 in RUNS:
            n = c1 - c0
            at = LAB_AT + c0 * CHUNK_WORDS if c1 < CHUNKS else LAB_AT + (c0 - 1) * CHUNK_FLOATS
            codes = placed.tile([P, n * P], U32, name=f"h_codes{c0}", align_bytes=ALIGN, offset=at)
            scales = keep.tile([P, n * P], U8, name=f"h_scales{c0}", align_bytes=ALIGN)
            nc.vector.quantize_mx(
                out=codes[:].bitcast(FP8X4),
                scales=scales[:],
                in_=h_bf[:, c0:c1, :, :].rearrange("p c n t -> p (c n t)"),
            )
            for i in range(n):
                h_mx.append((codes[:, i * P : (i + 1) * P], scales[:, i * P : (i + 1) * P]))

        res = [
            placed.tile([P, V], F32, name=f"res{c}", align_bytes=ALIGN, offset=LAB_AT + CHUNK_FLOATS if c == 0 else RES_AT + c * CHUNK_FLOATS)
            for c in range(CHUNKS)
        ]
        y_spare = psum.tile([P, V], F32, name="y_spare", tag="h0")
        for c in range(CHUNKS):
            images = slice(c * P, (c + 1) * P)
            banks = (y_acc[c], y_spare if c == 0 else y_acc[c])
            products = HALVES if c == 0 else 1
            for i in range(products):
                texts = slice(i * V // products, (i + 1) * V // products)
                nc.tensor.matmul_mx(
                    out=banks[i][:, texts],
                    lhsT=h_mx[c][0].bitcast(FP8X4),
                    lhsT_scale=h_mx[c][1],
                    rhs=ew[:, texts].bitcast(FP8X4),
                    rhs_scale=es[E_ROW:P, texts],
                    start=True,
                    stop=True,
                )
            th = keep.tile([P, V], F32, name=f"th{c}", align_bytes=ALIGN)
            store_halves = c in (0, CHUNKS - 1)
            for i in range(HALVES):
                texts = slice(i * V // HALVES, (i + 1) * V // HALVES)
                nc.scalar.activation(out=th[:, texts], in_=banks[i][:, texts], func=ACT.Tanh, bias=-0.25, scale=0.75)
                nc.vector.scalar_tensor_tensor(
                    out=res[c][:, texts], in0=th[:, texts], scalar=0.75, in1=shift[:, c, texts], op0=ALU.mult, op1=ALU.subtract
                )
                if store_halves:
                    nc.sync.dma_start(out=out[images, texts], in_=res[c][:, texts])
            if not store_halves:
                nc.sync.dma_start(out=out[images, :], in_=res[c][:])
